import numpy as np
import ml_dtypes


def mxq(x, axis, fmt="e4m3"):
    dtype, down = {"e4m3": (ml_dtypes.float8_e4m3fn, 7), "e5m2": (ml_dtypes.float8_e5m2, 14)}[fmt]
    v = np.moveaxis(np.asarray(x, np.float32).astype(ml_dtypes.bfloat16).astype(np.float64), axis, -1)
    blocks = v.reshape(v.shape[:-1] + (-1, 32))
    amax = np.abs(blocks).max(-1, keepdims=True)
    byte = np.maximum(np.where(amax > 0, np.frexp(amax)[1] - 1 + 127, 0) - down, 1)
    scale = np.exp2(byte - 127.0)
    codes = (blocks / scale).astype(np.float32).astype(dtype).astype(np.float64)
    return np.moveaxis((codes * scale).reshape(v.shape), -1, axis)


WIDE = False


def mx_kscale(k):
    if not WIDE:
        return np.ones(k)
    levels = np.array([10, -10, 5, -5, 0])
    if k % 512:
        return np.exp2(np.random.permutation(np.resize(levels, k // 32))).repeat(32)
    a = np.empty((k // 512, 16))
    for p in range(k // 512):
        a[p, :8] = np.random.permutation(np.resize(levels, 8))
        for g in range(8):
            far = levels[np.abs(levels - a[p, g]) >= 10]
            a[p, g + 8] = far[np.random.randint(len(far))]
    return np.exp2(a.ravel()).repeat(32)


def f64(x):
    return np.asarray(x).astype(np.float64)


def striped(idx):
    return np.tile(idx.reshape(-1, 16).T, (8, 1)).astype(np.uint16)


def unstriped(offs):
    return offs[:16].T.reshape(-1).astype(np.int64)


def pack_weight(w):
    k, n = w.shape
    w = f64(np.asarray(w, np.float32).astype(ml_dtypes.bfloat16)).reshape(k // 32, 32, n)
    amax = np.abs(w).max(1)
    byte = np.clip(np.where(amax > 0, np.frexp(amax)[1] - 1 + 127 - 7, 1), 1, 254)
    scaled = (w * np.exp2(127.0 - byte)[:, None, :]).reshape(k, n).astype(np.float32)
    words = np.ascontiguousarray(scaled.reshape(k // 512, 128, 4, n).transpose(0, 1, 3, 2)).astype(ml_dtypes.float8_e4m3fn).view(np.uint8)
    return words, np.ascontiguousarray(byte.astype(np.uint8).reshape(k // 512, 16, n))


def unpack_weight(words, scales):
    g, p, n, _ = words.shape
    vals = np.ascontiguousarray(words).view(ml_dtypes.float8_e4m3fn).astype(np.float64) * np.repeat(np.exp2(scales.astype(np.float64) - 127.0), 8, axis=1)[..., None]
    return vals.transpose(0, 1, 3, 2).reshape(g * 512, n)


E2M1 = np.array([0.0, 0.5, 1.0, 1.5, 2.0, 3.0, 4.0, 6.0, -0.0, -0.5, -1.0, -1.5, -2.0, -3.0, -4.0, -6.0])


def pack_fp4(w):
    k, n = w.shape
    w = f64(np.asarray(w, np.float32).astype(ml_dtypes.bfloat16)).reshape(k // 32, 32, n)
    amax = np.abs(w).max(1)
    mant, ex = np.frexp(amax / 6.0)
    byte = np.clip(np.where(amax > 0, np.where(mant > 0.5, ex, ex - 1) + 127, 1), 1, 254)
    scaled = (w * np.exp2(127.0 - byte)[:, None, :]).reshape(k, n).astype(np.float32)
    c = np.ascontiguousarray(scaled.reshape(k // 512, 128, 4, n).transpose(0, 1, 3, 2)).astype(ml_dtypes.float4_e2m1fn).view(np.uint8) & 0xF
    words = (c[..., 0::2] | (c[..., 1::2] << 4)).reshape(k // 512, 128, 2 * n)
    return np.ascontiguousarray(words), np.ascontiguousarray(byte.astype(np.uint8).reshape(k // 512, 16, n))


def unpack_fp4(words, scales):
    g, _, n = scales.shape
    words = np.ascontiguousarray(words).reshape(g, 128, n, 2)
    nib = np.empty((g, 128, n, 4), np.uint8)
    nib[..., 0::2] = words & 0xF
    nib[..., 1::2] = words >> 4
    vals = E2M1[nib] * np.repeat(np.exp2(scales.astype(np.float64) - 127.0), 8, axis=1)[..., None]
    return vals.transpose(0, 1, 3, 2).reshape(g * 512, n)


def silu(v):
    return v / (1.0 + np.exp(-np.maximum(v, -700.0)))


K, T, S, V, H, N = 512, 4096, 1024, 512, 512, 128


def setup_inputs():
    n = np.random.standard_normal
    s = mx_kscale(K)[:, None]
    u = mx_kscale(H)
    packed_xT = pack_weight(n((K, T)) * s)
    packed_w2 = pack_fp4(n((H, N)) / np.sqrt(3 * H) / u[:, None])
    packed_w3 = pack_fp4(n((H, N)) / np.sqrt(3 * H) / u[:, None])
    packed_w4 = pack_fp4(n((H, N)) / np.sqrt(3 * H) / u[:, None])
    return {
        "x_words": packed_xT[0],
        "x_scales": packed_xT[1],
        "w1": (n((K, H)) / np.sqrt(K) / s * u).astype(np.float32),
        "w2_words": packed_w2[0],
        "w2_scales": packed_w2[1],
        "w3_words": packed_w3[0],
        "w3_scales": packed_w3[1],
        "w4_words": packed_w4[0],
        "w4_scales": packed_w4[1],
        "offs": striped(np.random.permutation(T)[:S]),
        "pos1": striped(np.random.permutation(S)[:V]),
        "pos2": striped(np.random.permutation(S)[:V]),
        "pos3": striped(np.random.permutation(S)[:V]),
    }


def reference(x_words, x_scales, w1, w2_words, w2_scales, w3_words, w3_scales, w4_words, w4_scales, offs, pos1, pos2, pos3):
    xq = unpack_weight(x_words, x_scales)[:, unstriped(offs)]
    h = silu(mxq(f64(w1), 0, "e4m3").T @ xq)
    g0 = h[:, unstriped(pos1)]
    g1 = h[:, unstriped(pos2)]
    g2 = h[:, unstriped(pos3)]
    z1 = (g0 + g1 + g2) / 3
    z2 = np.maximum(np.maximum(g0, g1), g2)
    z3 = np.minimum(np.minimum(g0, g1), g2)
    return unpack_fp4(w2_words, w2_scales).T @ mxq(z1, 0, "e4m3") + unpack_fp4(w3_words, w3_scales).T @ mxq(z2, 0, "e4m3") + unpack_fp4(w4_words, w4_scales).T @ mxq(z3, 0, "e4m3")

@@ -1,0 +1,217 @@
+from contextlib import ExitStack
+
+import concourse.mybir as mybir
+from concourse.masks import make_identity
+
+K, T, S, V, H, N = 512, 4096, 1024, 512, 512, 128
+FLOPS = 2 * K * H * S + 3 * 2 * H * N * V
+
+F32 = mybir.dt.float32
+BF16 = mybir.dt.bfloat16
+I32 = mybir.dt.int32
+U32 = mybir.dt.uint32
+U16 = mybir.dt.uint16
+U8 = mybir.dt.uint8
+FP8X4 = mybir.dt.float8_e4m3fn_x4
+FP4X4 = mybir.dt.float4_e2m1fn_x4
+ACT = mybir.ActivationFunctionType
+ALU = mybir.AluOpType
+
+P = 128
+PACK = 4
+BANK = 512
+HALF = V // 2
+D = 3
+
+
+def load_scale_rows(queue, tile, rows):
+    for q in range(4):
+        queue.dma_start(out=tile[32 * q : 32 * q + 4, :].bitcast(I32), in_=rows[4 * q : 4 * q + 4, :].bitcast(I32))
+
+
+def tile_picked_pna_silu_p_kernel(
+    tc, x_words, x_scales, w1, w2_words, w2_scales, w3_words, w3_scales, w4_words, w4_scales, offs, pos1, pos2, pos3, out
+):
+    nc = tc.nc
+    with ExitStack() as ctx:
+        lists = ctx.enter_context(tc.tile_pool(name="lists", bufs=1))
+        keep = ctx.enter_context(tc.tile_pool(name="keep", bufs=1))
+        psum = ctx.enter_context(tc.psum_pool(name="psum", bufs=8))
+
+        def bank():
+            return psum.tile([P, BANK], F32, name="bank")
+
+        x_scale_table = keep.tile([P, T], U8, align_bytes=64)
+        nc.vector.memset(x_scale_table[:].bitcast(I32), 0)
+        w_scale_rows = keep.tile([P, D * N], U8, align_bytes=64)
+        nc.vector.memset(w_scale_rows[:].bitcast(I32), 0)
+
+        x_scale_rows = keep.tile([P, T], U8, align_bytes=64)
+        load_scale_rows(nc.sync, x_scale_rows, x_scales[0])
+        for q in range(4):
+            rows = slice(32 * q, 32 * q + 4)
+            nc.vector.tensor_copy(x_scale_table[rows, :].bitcast(I32), x_scale_rows[rows, :].bitcast(I32))
+        w1_raw = keep.tile([P, PACK, H], F32, align_bytes=64)
+        nc.sync.dma_start(out=w1_raw[:], in_=w1.rearrange("(p j) c -> p j c", j=PACK))
+        offs_list = lists.tile([P, S // 16], U16, name="offs_list")
+        nc.sync.dma_start(offs_list[:], offs)
+        x_word_table = keep.tile([P, T], I32, align_bytes=64)
+        nc.sync.dma_start(out=x_word_table[:], in_=x_words[0].rearrange("p n t -> p (n t)").bitcast(I32))
+        pos_lists = []
+        for d, pos in enumerate((pos1, pos2, pos3)):
+            pos_list = lists.tile([P, V // 16], U16, name="pos_list%d" % d)
+            nc.sync.dma_start(pos_list[:], pos)
+            pos_lists.append(pos_list)
+        w_words = []
+        for a, (words, scales) in enumerate(((w2_words, w2_scales), (w3_words, w3_scales), (w4_words, w4_scales))):
+            tile = keep.tile([P, 2 * N], U8, name="w_words%d" % a, align_bytes=64)
+            nc.sync.dma_start(out=tile[:].bitcast(I32), in_=words[0].bitcast(I32))
+            w_words.append(tile)
+            load_scale_rows(nc.sync, w_scale_rows[:, a * N : (a + 1) * N], scales[0])
+
+        identity = keep.tile([P, P], F32, align_bytes=64)
+        make_identity(nc, identity[:])
+
+        w1_bf = keep.tile([P, PACK, P, PACK], BF16, align_bytes=64)
+        nc.scalar.copy(
+            out=w1_bf[:].rearrange("p t m j -> p m j t"),
+            in_=w1_raw[:].rearrange("p j (m t) -> p m j t", t=PACK),
+        )
+        x_scale_picked = keep.tile([P, S], U8, align_bytes=64)
+        nc.vector.tensor_copy(x_scale_picked[:], x_scale_table[:].indirect(offs_list[:]))
+        w1_codes = keep.tile([P, H], U32, align_bytes=64)
+        w1_scales = keep.tile([P, H], U8, align_bytes=64)
+        nc.vector.quantize_mx(
+            out=w1_codes[:].bitcast(FP8X4), scales=w1_scales[:], in_=w1_bf[:].rearrange("p t m j -> p (t m j)")
+        )
+
+        x_picked = []
+        for s in range(S // BANK):
+            picked = keep.tile([P, BANK], U32, name="x_picked%d" % s, align_bytes=64)
+            nc.vector.tensor_copy(
+                picked[:], x_word_table[:].bitcast(U32).indirect(offs_list[:, s * BANK // 16 : (s + 1) * BANK // 16])
+            )
+            x_picked.append(picked)
+
+        h = []
+        for t in range(PACK):
+            h_t = keep.tile([P, S], F32, name="h%d" % t, align_bytes=64)
+            pieces = ((0, 0, BANK), (1, 0, HALF), (1, HALF, HALF)) if t == 0 else ((0, 0, BANK), (1, 0, BANK))
+            for s, first, width in pieces:
+                acc = bank()
+                cols = slice(s * BANK + first, s * BANK + first + width)
+                nc.tensor.matmul_mx(
+                    out=acc[:, 0:width],
+                    lhsT=w1_codes[:, t * P : (t + 1) * P].bitcast(FP8X4),
+                    lhsT_scale=w1_scales[:, t * P : (t + 1) * P],
+                    rhs=x_picked[s][:, first : first + width].bitcast(FP8X4),
+                    rhs_scale=x_scale_picked[:, cols],
+                    start=True,
+                    stop=True,
+                )
+                nc.scalar.activation(out=h_t[:, cols], in_=acc[:, 0:width], func=ACT.Silu)
+            h.append(h_t)
+
+        rounded = [keep.tile([P, 2, V, 2], BF16, name="rounded%d" % d, align_bytes=64) for d in range(D)]
+        mean_turned = [[None, None], [None, None]]
+        for u in range(2):
+            picked = [keep.tile([P, 2, V], F32, name="nbr%d_%d" % (u, d), align_bytes=64) for d in range(D)]
+            sums = [bank(), bank()]
+            for e in range(2):
+                for d in range(D):
+                    nc.vector.tensor_copy(picked[d][:, e, :], h[2 * u + e][:].indirect(pos_lists[d][:]))
+                for b in range(V // P):
+                    place = (2 * (b % 2) + e) * P
+                    for d in range(D):
+                        nc.tensor.matmul(
+                            sums[b // 2][:, place : place + P],
+                            picked[d][:, e, b * P : (b + 1) * P],
+                            identity[:],
+                            start=(d == 0),
+                            stop=(d == D - 1),
+                            is_transpose=True,
+                        )
+            for d in range(D):
+                for c in range(2):
+                    cols = slice(c * HALF, (c + 1) * HALF)
+                    nc.scalar.copy(out=rounded[d][:, u, cols, :], in_=picked[d][:, :, cols].rearrange("p e v -> p v e"))
+            for c in range(2):
+                turned = keep.tile([P, 2, P, 2], BF16, name="mean_turned%d_%d" % (u, c), align_bytes=64)
+                nc.scalar.activation(
+                    out=turned[:],
+                    in_=sums[c][:].rearrange("v (b e p) -> v b p e", b=2, e=2),
+                    func=ACT.Copy,
+                    scale=1.0 / D,
+                )
+                mean_turned[u][c] = turned
+
+        z = [[keep.tile([P, HALF, PACK], BF16, name="z%d_%d" % (a, c), align_bytes=64) for c in range(2)] for a in range(D)]
+        for c in range(2):
+            back = bank()
+            for u in range(2):
+                words = mean_turned[u][c][:].rearrange("v b p e -> v (b p e)").bitcast(F32)
+                for b in range(2):
+                    place = (2 * u + b) * P
+                    nc.tensor.transpose(back[:, place : place + P], words[:, b * P : (b + 1) * P], identity[:])
+            nc.scalar.copy(
+                out=z[0][c][:].rearrange("p v t -> p (v t)").bitcast(F32).rearrange("p (v u) -> p v u", u=2),
+                in_=back[:].rearrange("p (u v) -> p v u", u=2),
+            )
+
+        two = [keep.tile([P, 2, V, 2], BF16, name="two%d" % i, align_bytes=64) for i in range(2)]
+        ops = (ALU.max, ALU.min)
+        for u in range(2):
+            for i in range(2):
+                nc.vector.tensor_tensor(two[i][:, u], rounded[0][:, u], rounded[1][:, u], ops[i])
+
+        def last_extreme(i, c):
+            cols = slice(c * HALF, (c + 1) * HALF)
+            nc.vector.tensor_tensor(
+                z[1 + i][c][:].rearrange("p v (u e) -> p v u e", u=2),
+                two[i][:, :, cols, :].rearrange("p u v e -> p v u e"),
+                rounded[2][:, :, cols, :].rearrange("p u v e -> p v u e"),
+                ops[i],
+            )
+
+        accs = [bank() for b in range(V // P)]
+
+        def second_product(a, blocks, first, last):
+            c, width = blocks[0] // 2, len(blocks) * P
+            start = (blocks[0] % 2) * P
+            codes = keep.tile([P, width], U32, name="z_codes%d_%d" % (a, blocks[0]), align_bytes=64)
+            scales = keep.tile([P, width], U8, name="z_scales%d_%d" % (a, blocks[0]), align_bytes=64)
+            nc.vector.quantize_mx(
+                out=codes[:].bitcast(FP8X4),
+                scales=scales[:],
+                in_=z[a][c][:, start : start + width, :].rearrange("p v t -> p (v t)"),
+            )
+            for i, b in enumerate(blocks):
+                nc.tensor.matmul_mx(
+                    out=accs[b][:, 0:P],
+                    lhsT=w_words[a][:].bitcast(FP4X4),
+                    lhsT_scale=w_scale_rows[:, a * N : (a + 1) * N],
+                    rhs=codes[:, i * P : (i + 1) * P].bitcast(FP8X4),
+                    rhs_scale=scales[:, i * P : (i + 1) * P],
+                    start=first,
+                    stop=last,
+                )
+
+        def store(c, last_copy):
+            result = keep.tile([P, HALF], F32, name="result%d" % c, align_bytes=64)
+            nc.scalar.copy(out=result[:, 0:P], in_=accs[2 * c][:, 0:P])
+            last_copy(out=result[:, P:HALF], in_=accs[2 * c + 1][:, 0:P])
+            nc.sync.dma_start(out=out[:, c * HALF : (c + 1) * HALF], in_=result[:])
+
+        last_extreme(0, 0)
+        last_extreme(1, 0)
+        last_extreme(0, 1)
+        second_product(1, (0, 1), True, False)
+        second_product(2, (0, 1), False, False)
+        last_extreme(1, 1)
+        second_product(0, (0, 1), False, True)
+        store(0, nc.scalar.copy)
+        second_product(0, (2, 3), True, False)
+        second_product(1, (2, 3), False, False)
+        second_product(2, (2,), False, True)
+        second_product(2, (3,), False, True)
+        store(1, nc.vector.tensor_copy)

@@ -25,8 +25,8 @@ D = 3
 
 
 def load_scale_rows(queue, tile, rows):
-    for q in range(4):
-        queue.dma_start(out=tile[32 * q : 32 * q + 4, :].bitcast(I32), in_=rows[4 * q : 4 * q + 4, :].bitcast(I32))
+    for r in range(4):
+        queue.dma_start(out=tile[r:P:32, :].bitcast(I32), in_=rows[r:16:4, :].bitcast(I32))
 
 
 def tile_picked_pna_silu_p_kernel(
@@ -74,8 +74,8 @@ def tile_picked_pna_silu_p_kernel(
 
         w1_bf = keep.tile([P, PACK, P, PACK], BF16, align_bytes=64)
         nc.scalar.copy(
-            out=w1_bf[:].rearrange("p t m j -> p m j t"),
-            in_=w1_raw[:].rearrange("p j (m t) -> p m j t", t=PACK),
+            out=w1_bf[:].rearrange("p t m j -> p m t j"),
+            in_=w1_raw[:].rearrange("p j (m t) -> p m t j", t=PACK),
         )
         x_scale_picked = keep.tile([P, S], U8, align_bytes=64)
         nc.vector.tensor_copy(x_scale_picked[:], x_scale_table[:].indirect(offs_list[:]))
@@ -120,21 +120,18 @@ def tile_picked_pna_silu_p_kernel(
             for e in range(2):
                 for d in range(D):
                     nc.vector.tensor_copy(picked[d][:, e, :], h[2 * u + e][:].indirect(pos_lists[d][:]))
-                for b in range(V // P):
-                    place = (2 * (b % 2) + e) * P
-                    for d in range(D):
+                    for b in range(V // P):
+                        place = (2 * (b % 2) + e) * P
                         nc.tensor.matmul(
                             sums[b // 2][:, place : place + P],
                             picked[d][:, e, b * P : (b + 1) * P],
                             identity[:],
-                            start=(d == 0),
-                            stop=(d == D - 1),
+                            start=(e == 0 and d == 0 and b % 2 == 0),
+                            stop=(e == 1 and d == D - 1 and b % 2 == 1),
                             is_transpose=True,
                         )
             for d in range(D):
-                for c in range(2):
-                    cols = slice(c * HALF, (c + 1) * HALF)
-                    nc.scalar.copy(out=rounded[d][:, u, cols, :], in_=picked[d][:, :, cols].rearrange("p e v -> p v e"))
+                nc.scalar.copy(out=rounded[d][:, u], in_=picked[d][:].rearrange("p e v -> p v e"))
             for c in range(2):
                 turned = keep.tile([P, 2, P, 2], BF16, name="mean_turned%d_%d" % (u, c), align_bytes=64)
                 nc.scalar.activation(
@@ -145,7 +142,7 @@ def tile_picked_pna_silu_p_kernel(
                 )
                 mean_turned[u][c] = turned
 
-        z = [[keep.tile([P, HALF, PACK], BF16, name="z%d_%d" % (a, c), align_bytes=64) for c in range(2)] for a in range(D)]
+        z = [keep.tile([P, V, PACK], BF16, name="z%d" % a, align_bytes=64) for a in range(D)]
         for c in range(2):
             back = bank()
             for u in range(2):
@@ -153,37 +150,33 @@ def tile_picked_pna_silu_p_kernel(
                 for b in range(2):
                     place = (2 * u + b) * P
                     nc.tensor.transpose(back[:, place : place + P], words[:, b * P : (b + 1) * P], identity[:])
-            nc.scalar.copy(
-                out=z[0][c][:].rearrange("p v t -> p (v t)").bitcast(F32).rearrange("p (v u) -> p v u", u=2),
-                in_=back[:].rearrange("p (u v) -> p v u", u=2),
-            )
+            z_words = z[0][:, c * HALF : (c + 1) * HALF, :].rearrange("p v t -> p (v t)").bitcast(F32)
+            nc.scalar.copy(out=z_words.rearrange("p (v u) -> p v u", u=2), in_=back[:].rearrange("p (u v) -> p v u", u=2))
 
-        two = [keep.tile([P, 2, V, 2], BF16, name="two%d" % i, align_bytes=64) for i in range(2)]
-        ops = (ALU.max, ALU.min)
-        for u in range(2):
-            for i in range(2):
-                nc.vector.tensor_tensor(two[i][:, u], rounded[0][:, u], rounded[1][:, u], ops[i])
+        larger = keep.tile([P, 2, V, 2], BF16, align_bytes=64)
+        smaller = keep.tile([P, 2, V, 2], BF16, align_bytes=64)
+        nc.vector.tensor_tensor(larger[:, 0], rounded[0][:, 0], rounded[1][:, 0], ALU.max)
+        nc.vector.tensor_tensor(smaller[:], rounded[0][:], rounded[1][:], ALU.min)
+        nc.vector.tensor_tensor(larger[:, 1], rounded[0][:, 1], rounded[1][:, 1], ALU.max)
 
-        def last_extreme(i, c):
-            cols = slice(c * HALF, (c + 1) * HALF)
+        def with_third(a, two, op, cols):
             nc.vector.tensor_tensor(
-                z[1 + i][c][:].rearrange("p v (u e) -> p v u e", u=2),
-                two[i][:, :, cols, :].rearrange("p u v e -> p v u e"),
-                rounded[2][:, :, cols, :].rearrange("p u v e -> p v u e"),
-                ops[i],
+                z[a][:, cols].rearrange("p v (u e) -> p v u e", u=2),
+                two[:, :, cols].rearrange("p u v e -> p v u e"),
+                rounded[2][:, :, cols].rearrange("p u v e -> p v u e"),
+                op,
             )
 
         accs = [bank() for b in range(V // P)]
 
         def second_product(a, blocks, first, last):
-            c, width = blocks[0] // 2, len(blocks) * P
-            start = (blocks[0] % 2) * P
+            width = len(blocks) * P
             codes = keep.tile([P, width], U32, name="z_codes%d_%d" % (a, blocks[0]), align_bytes=64)
             scales = keep.tile([P, width], U8, name="z_scales%d_%d" % (a, blocks[0]), align_bytes=64)
             nc.vector.quantize_mx(
                 out=codes[:].bitcast(FP8X4),
                 scales=scales[:],
-                in_=z[a][c][:, start : start + width, :].rearrange("p v t -> p (v t)"),
+                in_=z[a][:, blocks[0] * P : blocks[0] * P + width, :].rearrange("p v t -> p (v t)"),
             )
             for i, b in enumerate(blocks):
                 nc.tensor.matmul_mx(
@@ -196,22 +189,17 @@ def tile_picked_pna_silu_p_kernel(
                     stop=last,
                 )
 
-        def store(c, last_copy):
-            result = keep.tile([P, HALF], F32, name="result%d" % c, align_bytes=64)
-            nc.scalar.copy(out=result[:, 0:P], in_=accs[2 * c][:, 0:P])
-            last_copy(out=result[:, P:HALF], in_=accs[2 * c + 1][:, 0:P])
-            nc.sync.dma_start(out=out[:, c * HALF : (c + 1) * HALF], in_=result[:])
+        def store(blocks, copy):
+            result = keep.tile([P, len(blocks) * P], F32, name="result%d" % blocks[0], align_bytes=64)
+            for i, b in enumerate(blocks):
+                copy(out=result[:, i * P : (i + 1) * P], in_=accs[b][:, 0:P])
+            nc.sync.dma_start(out=out[:, blocks[0] * P : (blocks[-1] + 1) * P], in_=result[:])
 
-        last_extreme(0, 0)
-        last_extreme(1, 0)
-        last_extreme(0, 1)
-        second_product(1, (0, 1), True, False)
-        second_product(2, (0, 1), False, False)
-        last_extreme(1, 1)
-        second_product(0, (0, 1), False, True)
-        store(0, nc.scalar.copy)
-        second_product(0, (2, 3), True, False)
-        second_product(1, (2, 3), False, False)
-        second_product(2, (2,), False, True)
-        second_product(2, (3,), False, True)
-        store(1, nc.vector.tensor_copy)
+        with_third(2, smaller, ALU.min, slice(0, V))
+        with_third(1, larger, ALU.max, slice(0, HALF))
+        second_product(2, (0, 1, 2, 3), True, False)
+        second_product(0, (0, 1, 2, 3), False, False)
+        with_third(1, larger, ALU.max, slice(HALF, V))
+        for blocks, copy in (((0, 1), nc.scalar.copy), ((2,), nc.scalar.copy), ((3,), nc.vector.tensor_copy)):
+            second_product(1, blocks, False, True)
+            store(blocks, copy)

@@ -36,6 +36,8 @@ def tile_picked_pna_silu_p_kernel(
     with ExitStack() as ctx:
         lists = ctx.enter_context(tc.tile_pool(name="lists", bufs=1))
         keep = ctx.enter_context(tc.tile_pool(name="keep", bufs=1))
+        reuse = ctx.enter_context(tc.tile_pool(name="reuse", bufs=1))
+        stage = ctx.enter_context(tc.tile_pool(name="stage", bufs=1))
         psum = ctx.enter_context(tc.psum_pool(name="psum", bufs=8))
 
         def bank():
@@ -43,48 +45,36 @@ def tile_picked_pna_silu_p_kernel(
 
         x_scale_table = keep.tile([P, T], U8, align_bytes=64)
         nc.vector.memset(x_scale_table[:].bitcast(I32), 0)
-        w_scale_rows = keep.tile([P, D * N], U8, align_bytes=64)
-        nc.vector.memset(w_scale_rows[:].bitcast(I32), 0)
 
-        x_scale_rows = keep.tile([P, T], U8, align_bytes=64)
-        load_scale_rows(nc.sync, x_scale_rows, x_scales[0])
-        for q in range(4):
-            rows = slice(32 * q, 32 * q + 4)
-            nc.vector.tensor_copy(x_scale_table[rows, :].bitcast(I32), x_scale_rows[rows, :].bitcast(I32))
-        w1_raw = keep.tile([P, PACK, H], F32, align_bytes=64)
-        nc.sync.dma_start(out=w1_raw[:], in_=w1.rearrange("(p j) c -> p j c", j=PACK))
+        x_scale_rows = keep.tile([16, T], U8, align_bytes=64)
+        nc.sync.dma_start(out=x_scale_rows[:].bitcast(I32), in_=x_scales[0].bitcast(I32))
+        nc.vector.tensor_copy(x_scale_table[0:16, :].bitcast(I32), x_scale_rows[:].bitcast(I32))
         offs_list = lists.tile([P, S // 16], U16, name="offs_list")
         nc.sync.dma_start(offs_list[:], offs)
         x_word_table = keep.tile([P, T], I32, align_bytes=64)
         nc.sync.dma_start(out=x_word_table[:], in_=x_words[0].rearrange("p n t -> p (n t)").bitcast(I32))
+        w1_raw = reuse.tile([P, PACK, H], F32, align_bytes=64, offset=0)
+        nc.sync.dma_start(out=w1_raw[:], in_=w1.rearrange("(p j) c -> p j c", j=PACK))
         pos_lists = []
         for d, pos in enumerate((pos1, pos2, pos3)):
             pos_list = lists.tile([P, V // 16], U16, name="pos_list%d" % d)
             nc.sync.dma_start(pos_list[:], pos)
             pos_lists.append(pos_list)
-        w_words = []
-        for a, (words, scales) in enumerate(((w2_words, w2_scales), (w3_words, w3_scales), (w4_words, w4_scales))):
-            tile = keep.tile([P, 2 * N], U8, name="w_words%d" % a, align_bytes=64)
-            nc.sync.dma_start(out=tile[:].bitcast(I32), in_=words[0].bitcast(I32))
-            w_words.append(tile)
-            load_scale_rows(nc.sync, w_scale_rows[:, a * N : (a + 1) * N], scales[0])
 
         identity = keep.tile([P, P], F32, align_bytes=64)
         make_identity(nc, identity[:])
+        warm = keep.tile([P, 1], F32, align_bytes=64)
+        nc.scalar.activation(out=warm[:], in_=identity[:, 0:1], func=ACT.Silu)
 
-        w1_bf = keep.tile([P, PACK, P, PACK], BF16, align_bytes=64)
-        nc.scalar.copy(
-            out=w1_bf[:].rearrange("p t m j -> p m t j"),
-            in_=w1_raw[:].rearrange("p j (m t) -> p m t j", t=PACK),
-        )
+        x_scale_gathered = keep.tile([P, S], U8, align_bytes=64)
+        nc.vector.tensor_copy(x_scale_gathered[:], x_scale_table[:].indirect(offs_list[:]))
         x_scale_picked = keep.tile([P, S], U8, align_bytes=64)
-        nc.vector.tensor_copy(x_scale_picked[:], x_scale_table[:].indirect(offs_list[:]))
-        w1_codes = keep.tile([P, H], U32, align_bytes=64)
-        w1_scales = keep.tile([P, H], U8, align_bytes=64)
-        nc.vector.quantize_mx(
-            out=w1_codes[:].bitcast(FP8X4), scales=w1_scales[:], in_=w1_bf[:].rearrange("p t m j -> p (t m j)")
-        )
-
+        nc.vector.tensor_copy(x_scale_picked[:].bitcast(I32), x_scale_gathered[:].bitcast(I32))
+        for q in range(1, 4):
+            nc.scalar.dma_start(
+                out=x_scale_picked[32 * q : 32 * q + 4, :].bitcast(I32),
+                in_=x_scale_gathered[4 * q : 4 * q + 4, :].bitcast(I32),
+            )
         x_picked = []
         for s in range(S // BANK):
             picked = keep.tile([P, BANK], U32, name="x_picked%d" % s, align_bytes=64)
@@ -93,17 +83,56 @@ def tile_picked_pna_silu_p_kernel(
             )
             x_picked.append(picked)
 
+        w1_bf = [
+            stage.tile([P, n, P, PACK], BF16, name="w1_bf%d" % u, align_bytes=64, offset=at)
+            for u, (n, at) in enumerate(((1, 0), (1, 4 * H), (2, 0)))
+        ]
+        w1_dealt = w1_raw[:].rearrange("p j (m t) -> p m t j", t=PACK)
+        w1_codes = []
+        w1_scales = []
+
+        def round_w1(copy, u, ms):
+            n = w1_bf[u].shape[1]
+            copy(out=w1_bf[u][:].rearrange("p e m j -> p m e j")[:, ms], in_=w1_dealt[:, ms, u : u + n, :])
+
+        def quantise_w1(u):
+            n = w1_bf[u].shape[1]
+            codes = keep.tile([P, n * P], U32, name="w1_codes%d" % u, align_bytes=64)
+            scales = keep.tile([P, n * P], U8, name="w1_scales%d" % u, align_bytes=64)
+            nc.vector.quantize_mx(
+                out=codes[:].bitcast(FP8X4), scales=scales[:], in_=w1_bf[u][:].rearrange("p e m j -> p (e m j)")
+            )
+            for i in range(n):
+                w1_codes.append(codes[:, i * P : (i + 1) * P])
+                w1_scales.append(scales[:, i * P : (i + 1) * P])
+
+        for u in range(2):
+            round_w1(nc.vector.tensor_copy, u, slice(0, P // 2))
+            round_w1(nc.scalar.copy, u, slice(P // 2, P))
+            quantise_w1(u)
+        round_w1(nc.vector.tensor_copy, 2, slice(0, P))
+        quantise_w1(2)
+
+        w_scale_rows = reuse.tile([P, D * N], U8, align_bytes=64, offset=D * 2 * N)
+        nc.vector.memset(w_scale_rows[:].bitcast(I32), 0)
+        w_words = []
+        for a, (words, scales) in enumerate(((w2_words, w2_scales), (w3_words, w3_scales), (w4_words, w4_scales))):
+            tile = reuse.tile([P, 2 * N], U8, name="w_words%d" % a, align_bytes=64, offset=a * 2 * N)
+            nc.sync.dma_start(out=tile[:].bitcast(I32), in_=words[0].bitcast(I32))
+            w_words.append(tile)
+            load_scale_rows(nc.sync, w_scale_rows[:, a * N : (a + 1) * N], scales[0])
+
         h = []
         for t in range(PACK):
             h_t = keep.tile([P, S], F32, name="h%d" % t, align_bytes=64)
-            pieces = ((0, 0, BANK), (1, 0, HALF), (1, HALF, HALF)) if t == 0 else ((0, 0, BANK), (1, 0, BANK))
+            pieces = ((0, 0, P), (0, P, P), (0, HALF, HALF), (1, 0, BANK)) if t == 0 else ((0, 0, BANK), (1, 0, BANK))
             for s, first, width in pieces:
                 acc = bank()
                 cols = slice(s * BANK + first, s * BANK + first + width)
                 nc.tensor.matmul_mx(
                     out=acc[:, 0:width],
-                    lhsT=w1_codes[:, t * P : (t + 1) * P].bitcast(FP8X4),
-                    lhsT_scale=w1_scales[:, t * P : (t + 1) * P],
+                    lhsT=w1_codes[t].bitcast(FP8X4),
+                    lhsT_scale=w1_scales[t],
                     rhs=x_picked[s][:, first : first + width].bitcast(FP8X4),
                     rhs_scale=x_scale_picked[:, cols],
                     start=True,

@@ -22,6 +22,7 @@ PACK = 4
 BANK = 512
 HALF = V // 2
 D = 3
+TOP = P - 16
 
 
 def load_scale_rows(queue, tile, rows):
@@ -44,22 +45,20 @@ def tile_picked_pna_silu_p_kernel(
             return psum.tile([P, BANK], F32, name="bank")
 
         x_scale_table = keep.tile([P, T], U8, align_bytes=64)
-        nc.vector.memset(x_scale_table[:].bitcast(I32), 0)
-
-        x_scale_rows = keep.tile([16, T], U8, align_bytes=64)
-        nc.sync.dma_start(out=x_scale_rows[:].bitcast(I32), in_=x_scales[0].bitcast(I32))
-        nc.vector.tensor_copy(x_scale_table[0:16, :].bitcast(I32), x_scale_rows[:].bitcast(I32))
+        nc.sync.dma_start(out=x_scale_table[TOP:P, :].bitcast(I32), in_=x_scales[0].bitcast(I32))
+        nc.vector.memset(x_scale_table[0:TOP, :].bitcast(I32), 0)
+        x_scale_picked = keep.tile([P, S], U8, align_bytes=64)
+        nc.vector.memset(x_scale_picked[:].bitcast(I32), 0)
         offs_list = lists.tile([P, S // 16], U16, name="offs_list")
         nc.sync.dma_start(offs_list[:], offs)
+        pos_lists = [lists.tile([P, V // 16], U16, name="pos_list%d" % d) for d in range(D)]
+        nc.sync.dma_start(pos_lists[0][:], pos1)
         x_word_table = keep.tile([P, T], I32, align_bytes=64)
         nc.sync.dma_start(out=x_word_table[:], in_=x_words[0].rearrange("p n t -> p (n t)").bitcast(I32))
         w1_raw = reuse.tile([P, PACK, H], F32, align_bytes=64, offset=0)
         nc.sync.dma_start(out=w1_raw[:], in_=w1.rearrange("(p j) c -> p j c", j=PACK))
-        pos_lists = []
-        for d, pos in enumerate((pos1, pos2, pos3)):
-            pos_list = lists.tile([P, V // 16], U16, name="pos_list%d" % d)
-            nc.sync.dma_start(pos_list[:], pos)
-            pos_lists.append(pos_list)
+        nc.sync.dma_start(pos_lists[1][:], pos2)
+        nc.sync.dma_start(pos_lists[2][:], pos3)
 
         identity = keep.tile([P, P], F32, align_bytes=64)
         make_identity(nc, identity[:])
@@ -68,12 +67,10 @@ def tile_picked_pna_silu_p_kernel(
 
         x_scale_gathered = keep.tile([P, S], U8, align_bytes=64)
         nc.vector.tensor_copy(x_scale_gathered[:], x_scale_table[:].indirect(offs_list[:]))
-        x_scale_picked = keep.tile([P, S], U8, align_bytes=64)
-        nc.vector.tensor_copy(x_scale_picked[:].bitcast(I32), x_scale_gathered[:].bitcast(I32))
-        for q in range(1, 4):
+        for q in range(4):
             nc.scalar.dma_start(
                 out=x_scale_picked[32 * q : 32 * q + 4, :].bitcast(I32),
-                in_=x_scale_gathered[4 * q : 4 * q + 4, :].bitcast(I32),
+                in_=x_scale_gathered[TOP + 4 * q : TOP + 4 * q + 4, :].bitcast(I32),
             )
         x_picked = []
         for s in range(S // BANK):
@@ -227,8 +224,11 @@ def tile_picked_pna_silu_p_kernel(
         with_third(2, smaller, ALU.min, slice(0, V))
         with_third(1, larger, ALU.max, slice(0, HALF))
         second_product(2, (0, 1, 2, 3), True, False)
-        second_product(0, (0, 1, 2, 3), False, False)
         with_third(1, larger, ALU.max, slice(HALF, V))
-        for blocks, copy in (((0, 1), nc.scalar.copy), ((2,), nc.scalar.copy), ((3,), nc.vector.tensor_copy)):
-            second_product(1, blocks, False, True)
+        second_product(1, (0, 1), False, False)
+        second_product(0, (0, 1), False, True)
+        store((0, 1), nc.scalar.copy)
+        second_product(1, (2, 3), False, False)
+        for blocks, copy in (((2,), nc.scalar.copy), ((3,), nc.vector.tensor_copy)):
+            second_product(0, blocks, False, True)
             store(blocks, copy)

@@ -52,11 +52,11 @@ def tile_picked_pna_silu_p_kernel(
         offs_list = lists.tile([P, S // 16], U16, name="offs_list")
         nc.sync.dma_start(offs_list[:], offs)
         pos_lists = [lists.tile([P, V // 16], U16, name="pos_list%d" % d) for d in range(D)]
-        nc.sync.dma_start(pos_lists[0][:], pos1)
         x_word_table = keep.tile([P, T], I32, align_bytes=64)
         nc.sync.dma_start(out=x_word_table[:], in_=x_words[0].rearrange("p n t -> p (n t)").bitcast(I32))
         w1_raw = reuse.tile([P, PACK, H], F32, align_bytes=64, offset=0)
         nc.sync.dma_start(out=w1_raw[:], in_=w1.rearrange("(p j) c -> p j c", j=PACK))
+        nc.sync.dma_start(pos_lists[0][:], pos1)
         nc.sync.dma_start(pos_lists[1][:], pos2)
         nc.sync.dma_start(pos_lists[2][:], pos3)
 
@@ -68,7 +68,7 @@ def tile_picked_pna_silu_p_kernel(
         x_scale_gathered = keep.tile([P, S], U8, align_bytes=64)
         nc.vector.tensor_copy(x_scale_gathered[:], x_scale_table[:].indirect(offs_list[:]))
         for q in range(4):
-            nc.scalar.dma_start(
+            nc.sync.dma_start(
                 out=x_scale_picked[32 * q : 32 * q + 4, :].bitcast(I32),
                 in_=x_scale_gathered[TOP + 4 * q : TOP + 4 * q + 4, :].bitcast(I32),
             )
@@ -122,7 +122,7 @@ def tile_picked_pna_silu_p_kernel(
         h = []
         for t in range(PACK):
             h_t = keep.tile([P, S], F32, name="h%d" % t, align_bytes=64)
-            pieces = ((0, 0, P), (0, P, P), (0, HALF, HALF), (1, 0, BANK)) if t == 0 else ((0, 0, BANK), (1, 0, BANK))
+            pieces = ((0, 0, HALF), (0, HALF, HALF), (1, 0, HALF), (1, HALF, P), (1, HALF + P, P)) if t == 0 else ((0, 0, BANK), (1, 0, BANK))
             for s, first, width in pieces:
                 acc = bank()
                 cols = slice(s * BANK + first, s * BANK + first + width)
@@ -224,11 +224,12 @@ def tile_picked_pna_silu_p_kernel(
         with_third(2, smaller, ALU.min, slice(0, V))
         with_third(1, larger, ALU.max, slice(0, HALF))
         second_product(2, (0, 1, 2, 3), True, False)
-        with_third(1, larger, ALU.max, slice(HALF, V))
         second_product(1, (0, 1), False, False)
         second_product(0, (0, 1), False, True)
         store((0, 1), nc.scalar.copy)
-        second_product(1, (2, 3), False, False)
+        second_product(0, (2, 3), False, False)
+        for b in (2, 3):
+            with_third(1, larger, ALU.max, slice(b * P, (b + 1) * P))
         for blocks, copy in (((2,), nc.scalar.copy), ((3,), nc.vector.tensor_copy)):
-            second_product(0, blocks, False, True)
+            second_product(1, blocks, False, True)
             store(blocks, copy)

@@ -54,8 +54,11 @@ def tile_picked_pna_silu_p_kernel(
         pos_lists = [lists.tile([P, V // 16], U16, name="pos_list%d" % d) for d in range(D)]
         x_word_table = keep.tile([P, T], I32, align_bytes=64)
         nc.sync.dma_start(out=x_word_table[:], in_=x_words[0].rearrange("p n t -> p (n t)").bitcast(I32))
-        w1_raw = reuse.tile([P, PACK, H], F32, align_bytes=64, offset=0)
-        nc.sync.dma_start(out=w1_raw[:], in_=w1.rearrange("(p j) c -> p j c", j=PACK))
+        w1_raw = []
+        for i in range(2):
+            rows = reuse.tile([P, 2, H], F32, name="w1_raw%d" % i, align_bytes=64, offset=(1 - i) * 2 * H * 4)
+            nc.sync.dma_start(out=rows[:], in_=w1.rearrange("(p j) c -> p j c", j=PACK)[:, 2 * i : 2 * i + 2, :])
+            w1_raw.append(rows)
         nc.sync.dma_start(pos_lists[0][:], pos1)
         nc.sync.dma_start(pos_lists[1][:], pos2)
         nc.sync.dma_start(pos_lists[2][:], pos3)
@@ -84,13 +87,16 @@ def tile_picked_pna_silu_p_kernel(
             stage.tile([P, n, P, PACK], BF16, name="w1_bf%d" % u, align_bytes=64, offset=at)
             for u, (n, at) in enumerate(((1, 0), (1, 4 * H), (2, 0)))
         ]
-        w1_dealt = w1_raw[:].rearrange("p j (m t) -> p m t j", t=PACK)
+        w1_dealt = [rows[:].rearrange("p j (m t) -> p m t j", t=PACK) for rows in w1_raw]
         w1_codes = []
         w1_scales = []
 
-        def round_w1(copy, u, ms):
+        def round_w1(copy, u, i, ms):
             n = w1_bf[u].shape[1]
-            copy(out=w1_bf[u][:].rearrange("p e m j -> p m e j")[:, ms], in_=w1_dealt[:, ms, u : u + n, :])
+            copy(
+                out=w1_bf[u][:].rearrange("p e m j -> p m e j")[:, ms, :, 2 * i : 2 * i + 2],
+                in_=w1_dealt[i][:, ms, u : u + n, :],
+            )
 
         def quantise_w1(u):
             n = w1_bf[u].shape[1]
@@ -104,10 +110,13 @@ def tile_picked_pna_silu_p_kernel(
                 w1_scales.append(scales[:, i * P : (i + 1) * P])
 
         for u in range(2):
-            round_w1(nc.vector.tensor_copy, u, slice(0, P // 2))
-            round_w1(nc.scalar.copy, u, slice(P // 2, P))
+            round_w1(nc.scalar.copy, u, 0, slice(0, P))
+        for u in range(2):
+            round_w1(nc.vector.tensor_copy, u, 1, slice(0, P // 2))
+            round_w1(nc.scalar.copy, u, 1, slice(P // 2, P))
             quantise_w1(u)
-        round_w1(nc.vector.tensor_copy, 2, slice(0, P))
+        for i in range(2):
+            round_w1(nc.vector.tensor_copy, 2, i, slice(0, P))
         quantise_w1(2)
 
         w_scale_rows = reuse.tile([P, D * N], U8, align_bytes=64, offset=D * 2 * N)

@@ -59,9 +59,6 @@ def tile_picked_pna_silu_p_kernel(
             rows = reuse.tile([P, 2, H], F32, name="w1_raw%d" % i, align_bytes=64, offset=(1 - i) * 2 * H * 4)
             nc.sync.dma_start(out=rows[:], in_=w1.rearrange("(p j) c -> p j c", j=PACK)[:, 2 * i : 2 * i + 2, :])
             w1_raw.append(rows)
-        nc.sync.dma_start(pos_lists[0][:], pos1)
-        nc.sync.dma_start(pos_lists[1][:], pos2)
-        nc.sync.dma_start(pos_lists[2][:], pos3)
 
         identity = keep.tile([P, P], F32, align_bytes=64)
         make_identity(nc, identity[:])
@@ -75,6 +72,9 @@ def tile_picked_pna_silu_p_kernel(
                 out=x_scale_picked[32 * q : 32 * q + 4, :].bitcast(I32),
                 in_=x_scale_gathered[TOP + 4 * q : TOP + 4 * q + 4, :].bitcast(I32),
             )
+        nc.sync.dma_start(pos_lists[0][:], pos1)
+        nc.sync.dma_start(pos_lists[1][:], pos2)
+        nc.sync.dma_start(pos_lists[2][:], pos3)
         x_picked = []
         for s in range(S // BANK):
             picked = keep.tile([P, BANK], U32, name="x_picked%d" % s, align_bytes=64)

@@ -39,7 +39,8 @@ def tile_picked_pna_silu_p_kernel(
         keep = ctx.enter_context(tc.tile_pool(name="keep", bufs=1))
         reuse = ctx.enter_context(tc.tile_pool(name="reuse", bufs=1))
         stage = ctx.enter_context(tc.tile_pool(name="stage", bufs=1))
-        psum = ctx.enter_context(tc.psum_pool(name="psum", bufs=8))
+        psum = ctx.enter_context(tc.psum_pool(name="psum", bufs=7))
+        psum_late = ctx.enter_context(tc.psum_pool(name="psum_late", bufs=1))
 
         def bank():
             return psum.tile([P, BANK], F32, name="bank")
@@ -179,7 +180,7 @@ def tile_picked_pna_silu_p_kernel(
 
         z = [keep.tile([P, V, PACK], BF16, name="z%d" % a, align_bytes=64) for a in range(D)]
         for c in range(2):
-            back = bank()
+            back = bank() if c else psum_late.tile([P, BANK], F32, name="late")
             for u in range(2):
                 words = mean_turned[u][c][:].rearrange("v b p e -> v (b p e)").bitcast(F32)
                 for b in range(2):
@@ -187,6 +188,18 @@ def tile_picked_pna_silu_p_kernel(
                     nc.tensor.transpose(back[:, place : place + P], words[:, b * P : (b + 1) * P], identity[:])
             z_words = z[0][:, c * HALF : (c + 1) * HALF, :].rearrange("p v t -> p (v t)").bitcast(F32)
             nc.scalar.copy(out=z_words.rearrange("p (v u) -> p v u", u=2), in_=back[:].rearrange("p (u v) -> p v u", u=2))
+
+        idle = psum_late.tile([P, BANK], F32, name="late")
+        for width in (BANK, BANK, HALF, P):
+            nc.tensor.matmul_mx(
+                out=idle[:, 0:width],
+                lhsT=w1_codes[0].bitcast(FP8X4),
+                lhsT_scale=w1_scales[0],
+                rhs=x_picked[0][:, 0:width].bitcast(FP8X4),
+                rhs_scale=x_scale_picked[:, 0:width],
+                start=True,
+                stop=True,
+            )
 
         larger = keep.tile([P, 2, V, 2], BF16, align_bytes=64)
         smaller = keep.tile([P, 2, V, 2], BF16, align_bytes=64)
@@ -231,14 +244,14 @@ def tile_picked_pna_silu_p_kernel(
             nc.sync.dma_start(out=out[:, blocks[0] * P : (blocks[-1] + 1) * P], in_=result[:])
 
         with_third(2, smaller, ALU.min, slice(0, V))
+        second_product(0, (0, 1), True, False)
+        second_product(2, (0, 1), False, False)
         with_third(1, larger, ALU.max, slice(0, HALF))
-        second_product(2, (0, 1, 2, 3), True, False)
-        second_product(1, (0, 1), False, False)
-        second_product(0, (0, 1), False, True)
+        second_product(0, (2, 3), True, False)
+        second_product(1, (0, 1), False, True)
         store((0, 1), nc.scalar.copy)
-        second_product(0, (2, 3), False, False)
-        for b in (2, 3):
-            with_third(1, larger, ALU.max, slice(b * P, (b + 1) * P))
+        with_third(1, larger, ALU.max, slice(HALF, V))
+        second_product(2, (2, 3), False, False)
         for blocks, copy in (((2,), nc.scalar.copy), ((3,), nc.vector.tensor_copy)):
             second_product(1, blocks, False, True)
             store(blocks, copy)

@@ -22,7 +22,7 @@ PACK = 4
 BANK = 512
 HALF = V // 2
 D = 3
-TOP = P - 16
+LEAD = 3 * T // 8
 
 
 def load_scale_rows(queue, tile, rows):
@@ -39,30 +39,34 @@ def tile_picked_pna_silu_p_kernel(
         keep = ctx.enter_context(tc.tile_pool(name="keep", bufs=1))
         reuse = ctx.enter_context(tc.tile_pool(name="reuse", bufs=1))
         stage = ctx.enter_context(tc.tile_pool(name="stage", bufs=1))
-        psum = ctx.enter_context(tc.psum_pool(name="psum", bufs=7))
-        psum_late = ctx.enter_context(tc.psum_pool(name="psum_late", bufs=1))
+        psum = ctx.enter_context(tc.psum_pool(name="psum", bufs=8))
 
         def bank():
             return psum.tile([P, BANK], F32, name="bank")
 
         x_scale_table = keep.tile([P, T], U8, align_bytes=64)
-        nc.sync.dma_start(out=x_scale_table[TOP:P, :].bitcast(I32), in_=x_scales[0].bitcast(I32))
-        nc.vector.memset(x_scale_table[0:TOP, :].bitcast(I32), 0)
+        nc.vector.memset(x_scale_table[:].bitcast(I32), 0)
+        identity = keep.tile([P, P], F32, align_bytes=64)
+        nc.vector.memset(identity[:], 0.0)
+        make_identity(nc, identity[:], nomemset=True)
         x_scale_picked = keep.tile([P, S], U8, align_bytes=64)
         nc.vector.memset(x_scale_picked[:].bitcast(I32), 0)
+        w_scale_rows = keep.tile([P, D * N], U8, align_bytes=64)
+        nc.vector.memset(w_scale_rows[:].bitcast(I32), 0)
+        x_word_table = keep.tile([P, T], I32, align_bytes=64)
+        x_word_rows = x_words[0].rearrange("p n t -> p (n t)").bitcast(I32)
+        nc.sync.dma_start(out=x_word_table[:, 0:LEAD], in_=x_word_rows[:, 0:LEAD])
         offs_list = lists.tile([P, S // 16], U16, name="offs_list")
         nc.sync.dma_start(offs_list[:], offs)
         pos_lists = [lists.tile([P, V // 16], U16, name="pos_list%d" % d) for d in range(D)]
-        x_word_table = keep.tile([P, T], I32, align_bytes=64)
-        nc.sync.dma_start(out=x_word_table[:], in_=x_words[0].rearrange("p n t -> p (n t)").bitcast(I32))
+        nc.sync.dma_start(out=x_scale_table[32:96:4, :].bitcast(I32), in_=x_scales[0].bitcast(I32))
+        nc.sync.dma_start(out=x_word_table[:, LEAD:T], in_=x_word_rows[:, LEAD:T])
         w1_raw = []
         for i in range(2):
             rows = reuse.tile([P, 2, H], F32, name="w1_raw%d" % i, align_bytes=64, offset=(1 - i) * 2 * H * 4)
             nc.sync.dma_start(out=rows[:], in_=w1.rearrange("(p j) c -> p j c", j=PACK)[:, 2 * i : 2 * i + 2, :])
             w1_raw.append(rows)
 
-        identity = keep.tile([P, P], F32, align_bytes=64)
-        make_identity(nc, identity[:])
         warm = keep.tile([P, 1], F32, align_bytes=64)
         nc.scalar.activation(out=warm[:], in_=identity[:, 0:1], func=ACT.Silu)
 
@@ -71,7 +75,7 @@ def tile_picked_pna_silu_p_kernel(
         for q in range(4):
             nc.sync.dma_start(
                 out=x_scale_picked[32 * q : 32 * q + 4, :].bitcast(I32),
-                in_=x_scale_gathered[TOP + 4 * q : TOP + 4 * q + 4, :].bitcast(I32),
+                in_=x_scale_gathered[32 + 16 * q : 48 + 16 * q : 4, :].bitcast(I32),
             )
         nc.sync.dma_start(pos_lists[0][:], pos1)
         nc.sync.dma_start(pos_lists[1][:], pos2)
@@ -112,19 +116,18 @@ def tile_picked_pna_silu_p_kernel(
 
         for u in range(2):
             round_w1(nc.scalar.copy, u, 0, slice(0, P))
-        for u in range(2):
-            round_w1(nc.vector.tensor_copy, u, 1, slice(0, P // 2))
-            round_w1(nc.scalar.copy, u, 1, slice(P // 2, P))
-            quantise_w1(u)
+        round_w1(nc.vector.tensor_copy, 0, 1, slice(0, P // 2))
+        round_w1(nc.scalar.copy, 0, 1, slice(P // 2, P))
+        round_w1(nc.scalar.copy, 1, 1, slice(0, P))
+        quantise_w1(0)
         for i in range(2):
             round_w1(nc.vector.tensor_copy, 2, i, slice(0, P))
+        quantise_w1(1)
         quantise_w1(2)
 
-        w_scale_rows = reuse.tile([P, D * N], U8, align_bytes=64, offset=D * 2 * N)
-        nc.vector.memset(w_scale_rows[:].bitcast(I32), 0)
         w_words = []
         for a, (words, scales) in enumerate(((w2_words, w2_scales), (w3_words, w3_scales), (w4_words, w4_scales))):
-            tile = reuse.tile([P, 2 * N], U8, name="w_words%d" % a, align_bytes=64, offset=a * 2 * N)
+            tile = keep.tile([P, 2 * N], U8, name="w_words%d" % a, align_bytes=64)
             nc.sync.dma_start(out=tile[:].bitcast(I32), in_=words[0].bitcast(I32))
             w_words.append(tile)
             load_scale_rows(nc.sync, w_scale_rows[:, a * N : (a + 1) * N], scales[0])
@@ -180,7 +183,7 @@ def tile_picked_pna_silu_p_kernel(
 
         z = [keep.tile([P, V, PACK], BF16, name="z%d" % a, align_bytes=64) for a in range(D)]
         for c in range(2):
-            back = bank() if c else psum_late.tile([P, BANK], F32, name="late")
+            back = bank()
             for u in range(2):
                 words = mean_turned[u][c][:].rearrange("v b p e -> v (b p e)").bitcast(F32)
                 for b in range(2):
@@ -188,18 +191,6 @@ def tile_picked_pna_silu_p_kernel(
                     nc.tensor.transpose(back[:, place : place + P], words[:, b * P : (b + 1) * P], identity[:])
             z_words = z[0][:, c * HALF : (c + 1) * HALF, :].rearrange("p v t -> p (v t)").bitcast(F32)
             nc.scalar.copy(out=z_words.rearrange("p (v u) -> p v u", u=2), in_=back[:].rearrange("p (u v) -> p v u", u=2))
-
-        idle = psum_late.tile([P, BANK], F32, name="late")
-        for width in (BANK, BANK, HALF, P):
-            nc.tensor.matmul_mx(
-                out=idle[:, 0:width],
-                lhsT=w1_codes[0].bitcast(FP8X4),
-                lhsT_scale=w1_scales[0],
-                rhs=x_picked[0][:, 0:width].bitcast(FP8X4),
-                rhs_scale=x_scale_picked[:, 0:width],
-                start=True,
-                stop=True,
-            )
 
         larger = keep.tile([P, 2, V, 2], BF16, align_bytes=64)
         smaller = keep.tile([P, 2, V, 2], BF16, align_bytes=64)

@@ -22,7 +22,7 @@ PACK = 4
 BANK = 512
 HALF = V // 2
 D = 3
-LEAD = 3 * T // 8
+LEAD = T // 4
 
 
 def load_scale_rows(queue, tile, rows):

@@ -151,52 +151,74 @@ def tile_picked_pna_silu_p_kernel(
                 nc.scalar.activation(out=h_t[:, cols], in_=acc[:, 0:width], func=ACT.Silu)
             h.append(h_t)
 
-        rounded = [keep.tile([P, 2, V, 2], BF16, name="rounded%d" % d, align_bytes=64) for d in range(D)]
-        mean_turned = [[None, None], [None, None]]
-        for u in range(2):
-            picked = [keep.tile([P, 2, V], F32, name="nbr%d_%d" % (u, d), align_bytes=64) for d in range(D)]
-            sums = [bank(), bank()]
-            for e in range(2):
-                for d in range(D):
-                    nc.vector.tensor_copy(picked[d][:, e, :], h[2 * u + e][:].indirect(pos_lists[d][:]))
-                    for b in range(V // P):
-                        place = (2 * (b % 2) + e) * P
-                        nc.tensor.matmul(
-                            sums[b // 2][:, place : place + P],
-                            picked[d][:, e, b * P : (b + 1) * P],
-                            identity[:],
-                            start=(e == 0 and d == 0 and b % 2 == 0),
-                            stop=(e == 1 and d == D - 1 and b % 2 == 1),
-                            is_transpose=True,
-                        )
-            for d in range(D):
-                nc.scalar.copy(out=rounded[d][:, u], in_=picked[d][:].rearrange("p e v -> p v e"))
-            for c in range(2):
-                turned = keep.tile([P, 2, P, 2], BF16, name="mean_turned%d_%d" % (u, c), align_bytes=64)
-                nc.scalar.activation(
-                    out=turned[:],
-                    in_=sums[c][:].rearrange("v (b e p) -> v b p e", b=2, e=2),
-                    func=ACT.Copy,
-                    scale=1.0 / D,
+        picked = [[keep.tile([P, 2, V], F32, name="nbr%d_%d" % (u, d), align_bytes=64) for d in range(D)] for u in range(2)]
+        sums = [[bank(), bank()], [bank(), bank()]]
+        added = {}
+
+        def fetch(on_vector, t, d, first, width):
+            u, e = divmod(t, 2)
+            into = picked[u][d][:, e, first : first + width]
+            found = h[t][:].indirect(pos_lists[d][:, first // 16 : (first + width) // 16])
+            if on_vector:
+                nc.vector.tensor_copy(into, found)
+            else:
+                nc.scalar.activation(out=into, in_=found, func=ACT.Copy)
+            for b in range(first // P, (first + width) // P):
+                count = added.get((u, b // 2), 0)
+                added[(u, b // 2)] = count + 1
+                place = (2 * (b % 2) + e) * P
+                nc.tensor.matmul(
+                    sums[u][b // 2][:, place : place + P],
+                    picked[u][d][:, e, b * P : (b + 1) * P],
+                    identity[:],
+                    start=(count == 0),
+                    stop=(count == 4 * D - 1),
+                    is_transpose=True,
                 )
-                mean_turned[u][c] = turned
+
+        for t, d in ((0, 0), (0, 1), (0, 2), (1, 0), (1, 1)):
+            fetch(True, t, d, 0, V)
+        fetch(False, 1, 2, 0, V)
+        for d in range(2):
+            for t in (2, 3):
+                fetch(False, t, d, 0, V)
+        for c in range(2):
+            for t in (2, 3):
+                fetch(False, t, 2, c * HALF, HALF)
 
         z = [keep.tile([P, V, PACK], BF16, name="z%d" % a, align_bytes=64) for a in range(D)]
+        turned = [
+            [keep.tile([P, 2, P, 2], BF16, name="mean_turned%d_%d" % (u, c), align_bytes=64) for c in range(2)] for u in range(2)
+        ]
+        backs = []
         for c in range(2):
             back = bank()
             for u in range(2):
-                words = mean_turned[u][c][:].rearrange("v b p e -> v (b p e)").bitcast(F32)
+                nc.scalar.activation(
+                    out=turned[u][c][:],
+                    in_=sums[u][c][:].rearrange("v (b e p) -> v b p e", b=2, e=2),
+                    func=ACT.Copy,
+                    scale=1.0 / D,
+                )
+                words = turned[u][c][:].rearrange("v b p e -> v (b p e)").bitcast(F32)
                 for b in range(2):
                     place = (2 * u + b) * P
                     nc.tensor.transpose(back[:, place : place + P], words[:, b * P : (b + 1) * P], identity[:])
+            backs.append(back)
+        for c in range(2):
             z_words = z[0][:, c * HALF : (c + 1) * HALF, :].rearrange("p v t -> p (v t)").bitcast(F32)
-            nc.scalar.copy(out=z_words.rearrange("p (v u) -> p v u", u=2), in_=back[:].rearrange("p (u v) -> p v u", u=2))
+            nc.scalar.copy(out=z_words.rearrange("p (v u) -> p v u", u=2), in_=backs[c][:].rearrange("p (u v) -> p v u", u=2))
 
+        rounded = [keep.tile([P, 2, V, 2], BF16, name="rounded%d" % d, align_bytes=64) for d in range(D)]
         larger = keep.tile([P, 2, V, 2], BF16, align_bytes=64)
         smaller = keep.tile([P, 2, V, 2], BF16, align_bytes=64)
-        nc.vector.tensor_tensor(larger[:, 0], rounded[0][:, 0], rounded[1][:, 0], ALU.max)
-        nc.vector.tensor_tensor(smaller[:], rounded[0][:], rounded[1][:], ALU.min)
-        nc.vector.tensor_tensor(larger[:, 1], rounded[0][:, 1], rounded[1][:, 1], ALU.max)
+
+        def round_pair(u, d, cols):
+            nc.vector.tensor_copy(out=rounded[d][:, u, cols], in_=picked[u][d][:, :, cols].rearrange("p e v -> p v e"))
+
+        def of_two(u):
+            nc.vector.tensor_tensor(larger[:, u], rounded[0][:, u], rounded[1][:, u], ALU.max)
+            nc.vector.tensor_tensor(smaller[:, u], rounded[0][:, u], rounded[1][:, u], ALU.min)
 
         def with_third(a, two, op, cols):
             nc.vector.tensor_tensor(
@@ -206,43 +228,58 @@ def tile_picked_pna_silu_p_kernel(
                 op,
             )
 
-        accs = [bank() for b in range(V // P)]
-
-        def second_product(a, blocks, first, last):
-            width = len(blocks) * P
-            codes = keep.tile([P, width], U32, name="z_codes%d_%d" % (a, blocks[0]), align_bytes=64)
-            scales = keep.tile([P, width], U8, name="z_scales%d_%d" % (a, blocks[0]), align_bytes=64)
+        def quantise_z(a, c):
+            codes = keep.tile([P, HALF], U32, name="z_codes%d_%d" % (a, c), align_bytes=64)
+            scales = keep.tile([P, HALF], U8, name="z_scales%d_%d" % (a, c), align_bytes=64)
             nc.vector.quantize_mx(
                 out=codes[:].bitcast(FP8X4),
                 scales=scales[:],
-                in_=z[a][:, blocks[0] * P : blocks[0] * P + width, :].rearrange("p v t -> p (v t)"),
+                in_=z[a][:, c * HALF : (c + 1) * HALF, :].rearrange("p v t -> p (v t)"),
             )
-            for i, b in enumerate(blocks):
+            return codes, scales
+
+        accs = [bank() for b in range(3)]
+        groups = (((0, 0, HALF),), ((1, 0, P), (2, P, P)))
+
+        def second_product(a, c, first, last):
+            codes, scales = quantise_z(a, c)
+            for g, at, width in groups[c]:
                 nc.tensor.matmul_mx(
-                    out=accs[b][:, 0:P],
+                    out=accs[g][:, 0:width],
                     lhsT=w_words[a][:].bitcast(FP4X4),
                     lhsT_scale=w_scale_rows[:, a * N : (a + 1) * N],
-                    rhs=codes[:, i * P : (i + 1) * P].bitcast(FP8X4),
-                    rhs_scale=scales[:, i * P : (i + 1) * P],
+                    rhs=codes[:, at : at + width].bitcast(FP8X4),
+                    rhs_scale=scales[:, at : at + width],
                     start=first,
                     stop=last,
                 )
 
-        def store(blocks, copy):
-            result = keep.tile([P, len(blocks) * P], F32, name="result%d" % blocks[0], align_bytes=64)
-            for i, b in enumerate(blocks):
-                copy(out=result[:, i * P : (i + 1) * P], in_=accs[b][:, 0:P])
-            nc.sync.dma_start(out=out[:, blocks[0] * P : (blocks[-1] + 1) * P], in_=result[:])
+        def store(g, first, width, copy):
+            result = keep.tile([P, width], F32, name="result%d" % g, align_bytes=64)
+            copy(out=result[:], in_=accs[g][:, 0:width])
+            nc.sync.dma_start(out=out[:, first : first + width], in_=result[:])
 
-        with_third(2, smaller, ALU.min, slice(0, V))
-        second_product(0, (0, 1), True, False)
-        second_product(2, (0, 1), False, False)
-        with_third(1, larger, ALU.max, slice(0, HALF))
-        second_product(0, (2, 3), True, False)
-        second_product(1, (0, 1), False, True)
-        store((0, 1), nc.scalar.copy)
-        with_third(1, larger, ALU.max, slice(HALF, V))
-        second_product(2, (2, 3), False, False)
-        for blocks, copy in (((2,), nc.scalar.copy), ((3,), nc.vector.tensor_copy)):
-            second_product(1, blocks, False, True)
-            store(blocks, copy)
+        every = slice(0, V)
+        halves = (slice(0, HALF), slice(HALF, V))
+        round_pair(0, 0, every)
+        round_pair(0, 1, every)
+        round_pair(0, 2, every)
+        of_two(0)
+        round_pair(1, 0, every)
+        round_pair(1, 1, every)
+        of_two(1)
+        round_pair(1, 2, halves[0])
+        with_third(1, larger, ALU.max, halves[0])
+        with_third(2, smaller, ALU.min, halves[0])
+        round_pair(1, 2, halves[1])
+        second_product(1, 0, True, False)
+        second_product(2, 0, False, False)
+        with_third(1, larger, ALU.max, halves[1])
+        with_third(2, smaller, ALU.min, halves[1])
+        second_product(1, 1, True, False)
+        second_product(0, 0, False, True)
+        store(0, 0, HALF, nc.scalar.copy)
+        second_product(2, 1, False, False)
+        second_product(0, 1, False, True)
+        store(1, HALF, P, nc.scalar.copy)
+        store(2, HALF + P, P, nc.vector.tensor_copy)

@@ -151,7 +151,11 @@ def tile_picked_pna_silu_p_kernel(
                 nc.scalar.activation(out=h_t[:, cols], in_=acc[:, 0:width], func=ACT.Silu)
             h.append(h_t)
 
-        picked = [[keep.tile([P, 2, V], F32, name="nbr%d_%d" % (u, d), align_bytes=64) for d in range(D)] for u in range(2)]
+        last_list = keep.tile([P, 2, 2, V], F32, align_bytes=64)
+        picked = [
+            [keep.tile([P, 2, V], F32, name="nbr%d_%d" % (u, d), align_bytes=64)[:] for d in range(2)] + [last_list[:, u]]
+            for u in range(2)
+        ]
         sums = [[bank(), bank()], [bank(), bank()]]
         added = {}
 
@@ -176,12 +180,10 @@ def tile_picked_pna_silu_p_kernel(
                     is_transpose=True,
                 )
 
-        for t, d in ((0, 0), (0, 1), (0, 2), (1, 0), (1, 1)):
+        for t, d in ((0, 0), (0, 1), (1, 0), (1, 1), (2, 0), (3, 0)):
             fetch(True, t, d, 0, V)
-        fetch(False, 1, 2, 0, V)
-        for d in range(2):
-            for t in (2, 3):
-                fetch(False, t, d, 0, V)
+        for t, d in ((0, 2), (1, 2), (2, 1), (3, 1)):
+            fetch(False, t, d, 0, V)
         for c in range(2):
             for t in (2, 3):
                 fetch(False, t, 2, c * HALF, HALF)
@@ -209,22 +211,30 @@ def tile_picked_pna_silu_p_kernel(
             z_words = z[0][:, c * HALF : (c + 1) * HALF, :].rearrange("p v t -> p (v t)").bitcast(F32)
             nc.scalar.copy(out=z_words.rearrange("p (v u) -> p v u", u=2), in_=backs[c][:].rearrange("p (u v) -> p v u", u=2))
 
-        rounded = [keep.tile([P, 2, V, 2], BF16, name="rounded%d" % d, align_bytes=64) for d in range(D)]
+        third = keep.tile([P, 2, V, 2], BF16, align_bytes=64)
         larger = keep.tile([P, 2, V, 2], BF16, align_bytes=64)
         smaller = keep.tile([P, 2, V, 2], BF16, align_bytes=64)
 
-        def round_pair(u, d, cols):
-            nc.vector.tensor_copy(out=rounded[d][:, u, cols], in_=picked[u][d][:, :, cols].rearrange("p e v -> p v e"))
+        rounded = [keep.tile([P, V, 2], BF16, name="rounded%d" % d, align_bytes=64) for d in range(2)]
+        for d in range(2):
+            nc.gpsimd.tensor_scalar(rounded[d][:], picked[0][d].rearrange("p e v -> p v e"), 1.0, 0.0, ALU.mult, ALU.add)
+        nc.gpsimd.tensor_scalar(
+            third[:, 0, 0:HALF], last_list[:, 0, :, 0:HALF].rearrange("p e v -> p v e"), 1.0, 0.0, ALU.mult, ALU.add
+        )
 
         def of_two(u):
-            nc.vector.tensor_tensor(larger[:, u], rounded[0][:, u], rounded[1][:, u], ALU.max)
-            nc.vector.tensor_tensor(smaller[:, u], rounded[0][:, u], rounded[1][:, u], ALU.min)
+            if u == 0:
+                first, second = rounded[0][:], rounded[1][:]
+            else:
+                first, second = (picked[u][d].rearrange("p e v -> p v e") for d in range(2))
+            nc.vector.tensor_tensor(larger[:, u], first, second, ALU.max)
+            nc.vector.tensor_tensor(smaller[:, u], first, second, ALU.min)
 
         def with_third(a, two, op, cols):
             nc.vector.tensor_tensor(
                 z[a][:, cols].rearrange("p v (u e) -> p v u e", u=2),
                 two[:, :, cols].rearrange("p u v e -> p v u e"),
-                rounded[2][:, :, cols].rearrange("p u v e -> p v u e"),
+                third[:, :, cols].rearrange("p u v e -> p v u e"),
                 op,
             )
 
@@ -259,19 +269,13 @@ def tile_picked_pna_silu_p_kernel(
             copy(out=result[:], in_=accs[g][:, 0:width])
             nc.sync.dma_start(out=out[:, first : first + width], in_=result[:])
 
-        every = slice(0, V)
         halves = (slice(0, HALF), slice(HALF, V))
-        round_pair(0, 0, every)
-        round_pair(0, 1, every)
-        round_pair(0, 2, every)
         of_two(0)
-        round_pair(1, 0, every)
-        round_pair(1, 1, every)
         of_two(1)
-        round_pair(1, 2, halves[0])
+        nc.vector.tensor_copy(out=third[:, 1, halves[0]], in_=last_list[:, 1, :, halves[0]].rearrange("p e v -> p v e"))
         with_third(1, larger, ALU.max, halves[0])
         with_third(2, smaller, ALU.min, halves[0])
-        round_pair(1, 2, halves[1])
+        nc.vector.tensor_copy(out=third[:, :, halves[1]], in_=last_list[:, :, :, halves[1]].rearrange("p u e v -> p u v e"))
         second_product(1, 0, True, False)
         second_product(2, 0, False, False)
         with_third(1, larger, ALU.max, halves[1])

@@ -180,110 +180,112 @@ def tile_picked_pna_silu_p_kernel(
                     is_transpose=True,
                 )
 
-        for t, d in ((0, 0), (0, 1), (1, 0), (1, 1), (2, 0), (3, 0)):
+        for t, d in ((0, 0), (0, 1), (1, 0), (1, 1), (2, 0)):
             fetch(True, t, d, 0, V)
-        for t, d in ((0, 2), (1, 2), (2, 1), (3, 1)):
+        fetch(True, 3, 0, 0, V - P)
+        fetch(False, 3, 0, V - P, P)
+        for t, d in ((2, 1), (3, 1), (0, 2), (1, 2)):
             fetch(False, t, d, 0, V)
-        for c in range(2):
+        for first in (0, HALF):
             for t in (2, 3):
-                fetch(False, t, 2, c * HALF, HALF)
+                fetch(False, t, 2, first, HALF)
 
-        z = [keep.tile([P, V, PACK], BF16, name="z%d" % a, align_bytes=64) for a in range(D)]
-        turned = [
-            [keep.tile([P, 2, P, 2], BF16, name="mean_turned%d_%d" % (u, c), align_bytes=64) for c in range(2)] for u in range(2)
-        ]
+        z_mean = keep.tile([P, V, PACK], BF16, align_bytes=64)
+        z_ends = [keep.tile([P, 2, HALF, PACK], BF16, name="z_ends%d" % c, align_bytes=64) for c in range(2)]
         backs = []
         for c in range(2):
             back = bank()
             for u in range(2):
+                turned = keep.tile([P, 2, P, 2], BF16, name="mean_turned%d_%d" % (u, c), align_bytes=64)
                 nc.scalar.activation(
-                    out=turned[u][c][:],
+                    out=turned[:],
                     in_=sums[u][c][:].rearrange("v (b e p) -> v b p e", b=2, e=2),
                     func=ACT.Copy,
                     scale=1.0 / D,
                 )
-                words = turned[u][c][:].rearrange("v b p e -> v (b p e)").bitcast(F32)
+                words = turned[:].rearrange("v b p e -> v (b p e)").bitcast(F32)
                 for b in range(2):
                     place = (2 * u + b) * P
                     nc.tensor.transpose(back[:, place : place + P], words[:, b * P : (b + 1) * P], identity[:])
             backs.append(back)
+        halves = (slice(0, HALF), slice(HALF, V))
         for c in range(2):
-            z_words = z[0][:, c * HALF : (c + 1) * HALF, :].rearrange("p v t -> p (v t)").bitcast(F32)
+            z_words = z_mean[:, halves[c], :].rearrange("p v t -> p (v t)").bitcast(F32)
             nc.scalar.copy(out=z_words.rearrange("p (v u) -> p v u", u=2), in_=backs[c][:].rearrange("p (u v) -> p v u", u=2))
 
         third = keep.tile([P, 2, V, 2], BF16, align_bytes=64)
         larger = keep.tile([P, 2, V, 2], BF16, align_bytes=64)
         smaller = keep.tile([P, 2, V, 2], BF16, align_bytes=64)
-
         rounded = [keep.tile([P, V, 2], BF16, name="rounded%d" % d, align_bytes=64) for d in range(2)]
         for d in range(2):
             nc.gpsimd.tensor_scalar(rounded[d][:], picked[0][d].rearrange("p e v -> p v e"), 1.0, 0.0, ALU.mult, ALU.add)
-        nc.gpsimd.tensor_scalar(
-            third[:, 0, 0:HALF], last_list[:, 0, :, 0:HALF].rearrange("p e v -> p v e"), 1.0, 0.0, ALU.mult, ALU.add
-        )
 
-        def of_two(u):
-            if u == 0:
-                first, second = rounded[0][:], rounded[1][:]
-            else:
-                first, second = (picked[u][d].rearrange("p e v -> p v e") for d in range(2))
-            nc.vector.tensor_tensor(larger[:, u], first, second, ALU.max)
-            nc.vector.tensor_tensor(smaller[:, u], first, second, ALU.min)
+        def round_third(u, cols):
+            nc.vector.tensor_copy(out=third[:, u, cols], in_=last_list[:, u, :, cols].rearrange("p e v -> p v e"))
 
-        def with_third(a, two, op, cols):
+        def first_pair_of_two(two, op):
+            nc.vector.tensor_tensor(two[:, 0], rounded[0][:], rounded[1][:], op)
+
+        def second_pair_of_two(two, op, cols):
+            first, second = (picked[1][d][:, :, cols].rearrange("p e v -> p v e") for d in range(2))
+            nc.vector.tensor_tensor(two[:, 1, cols], first, second, op)
+
+        def with_third(a, two, op, c):
             nc.vector.tensor_tensor(
-                z[a][:, cols].rearrange("p v (u e) -> p v u e", u=2),
-                two[:, :, cols].rearrange("p u v e -> p v u e"),
-                third[:, :, cols].rearrange("p u v e -> p v u e"),
+                z_ends[c][:, a].rearrange("p v (u e) -> p v u e", u=2),
+                two[:, :, halves[c]].rearrange("p u v e -> p v u e"),
+                third[:, :, halves[c]].rearrange("p u v e -> p v u e"),
                 op,
             )
-
-        def quantise_z(a, c):
-            codes = keep.tile([P, HALF], U32, name="z_codes%d_%d" % (a, c), align_bytes=64)
-            scales = keep.tile([P, HALF], U8, name="z_scales%d_%d" % (a, c), align_bytes=64)
-            nc.vector.quantize_mx(
-                out=codes[:].bitcast(FP8X4),
-                scales=scales[:],
-                in_=z[a][:, c * HALF : (c + 1) * HALF, :].rearrange("p v t -> p (v t)"),
-            )
-            return codes, scales
 
         accs = [bank() for b in range(3)]
         groups = (((0, 0, HALF),), ((1, 0, P), (2, P, P)))
 
-        def second_product(a, c, first, last):
-            codes, scales = quantise_z(a, c)
-            for g, at, width in groups[c]:
-                nc.tensor.matmul_mx(
-                    out=accs[g][:, 0:width],
-                    lhsT=w_words[a][:].bitcast(FP4X4),
-                    lhsT_scale=w_scale_rows[:, a * N : (a + 1) * N],
-                    rhs=codes[:, at : at + width].bitcast(FP8X4),
-                    rhs_scale=scales[:, at : at + width],
-                    start=first,
-                    stop=last,
-                )
+        def second_product(values, matrices, c, start, stop):
+            width = len(matrices) * HALF
+            codes = keep.tile([P, width], U32, name="z_codes%d_%d" % (matrices[0], c), align_bytes=64)
+            scales = keep.tile([P, width], U8, name="z_scales%d_%d" % (matrices[0], c), align_bytes=64)
+            nc.vector.quantize_mx(out=codes[:].bitcast(FP8X4), scales=scales[:], in_=values)
+            for i, a in enumerate(matrices):
+                for g, at, cols in groups[c]:
+                    span = slice(i * HALF + at, i * HALF + at + cols)
+                    nc.tensor.matmul_mx(
+                        out=accs[g][:, 0:cols],
+                        lhsT=w_words[a][:].bitcast(FP4X4),
+                        lhsT_scale=w_scale_rows[:, a * N : (a + 1) * N],
+                        rhs=codes[:, span].bitcast(FP8X4),
+                        rhs_scale=scales[:, span],
+                        start=start and i == 0,
+                        stop=stop and i == len(matrices) - 1,
+                    )
+
+        def ends_product(c, start, stop):
+            second_product(z_ends[c][:].rearrange("p a v t -> p (a v t)"), (1, 2), c, start, stop)
+
+        def mean_product(c, start, stop):
+            second_product(z_mean[:, halves[c], :].rearrange("p v t -> p (v t)"), (0,), c, start, stop)
 
         def store(g, first, width, copy):
             result = keep.tile([P, width], F32, name="result%d" % g, align_bytes=64)
             copy(out=result[:], in_=accs[g][:, 0:width])
             nc.sync.dma_start(out=out[:, first : first + width], in_=result[:])
 
-        halves = (slice(0, HALF), slice(HALF, V))
-        of_two(0)
-        of_two(1)
-        nc.vector.tensor_copy(out=third[:, 1, halves[0]], in_=last_list[:, 1, :, halves[0]].rearrange("p e v -> p v e"))
-        with_third(1, larger, ALU.max, halves[0])
-        with_third(2, smaller, ALU.min, halves[0])
-        nc.vector.tensor_copy(out=third[:, :, halves[1]], in_=last_list[:, :, :, halves[1]].rearrange("p u e v -> p u v e"))
-        second_product(1, 0, True, False)
-        second_product(2, 0, False, False)
-        with_third(1, larger, ALU.max, halves[1])
-        with_third(2, smaller, ALU.min, halves[1])
-        second_product(1, 1, True, False)
-        second_product(0, 0, False, True)
+        first_pair_of_two(larger, ALU.max)
+        first_pair_of_two(smaller, ALU.min)
+        second_pair_of_two(larger, ALU.max, slice(0, V))
+        round_third(0, slice(0, V))
+        second_pair_of_two(smaller, ALU.min, halves[0])
+        round_third(1, halves[0])
+        second_pair_of_two(smaller, ALU.min, halves[1])
+        with_third(0, larger, ALU.max, 0)
+        with_third(1, smaller, ALU.min, 0)
+        round_third(1, halves[1])
+        ends_product(0, True, False)
+        with_third(0, larger, ALU.max, 1)
+        with_third(1, smaller, ALU.min, 1)
+        mean_product(0, False, True)
         store(0, 0, HALF, nc.scalar.copy)
-        second_product(2, 1, False, False)
-        second_product(0, 1, False, True)
+        ends_product(1, True, False)
+        mean_product(1, False, True)
         store(1, HALF, P, nc.scalar.copy)
         store(2, HALF + P, P, nc.vector.tensor_copy)

@@ -23,6 +23,7 @@ BANK = 512
 HALF = V // 2
 D = 3
 LEAD = T // 4
+LINE = 4
 
 
 def load_scale_rows(queue, tile, rows):
@@ -190,8 +191,7 @@ def tile_picked_pna_silu_p_kernel(
             for t in (2, 3):
                 fetch(False, t, 2, first, HALF)
 
-        z_mean = keep.tile([P, V, PACK], BF16, align_bytes=64)
-        z_ends = [keep.tile([P, 2, HALF, PACK], BF16, name="z_ends%d" % c, align_bytes=64) for c in range(2)]
+        z = [keep.tile([P, V, PACK], BF16, name="z%d" % a, align_bytes=64) for a in range(D)]
         backs = []
         for c in range(2):
             back = bank()
@@ -209,9 +209,14 @@ def tile_picked_pna_silu_p_kernel(
                     nc.tensor.transpose(back[:, place : place + P], words[:, b * P : (b + 1) * P], identity[:])
             backs.append(back)
         halves = (slice(0, HALF), slice(HALF, V))
-        for c in range(2):
-            z_words = z_mean[:, halves[c], :].rearrange("p v t -> p (v t)").bitcast(F32)
-            nc.scalar.copy(out=z_words.rearrange("p (v u) -> p v u", u=2), in_=backs[c][:].rearrange("p (u v) -> p v u", u=2))
+        pieces = ((0, HALF), (HALF, P), (HALF + P, P))
+        for first, width in pieces:
+            c, at = divmod(first, HALF)
+            z_words = z[0][:, first : first + width, :].rearrange("p v t -> p (v t)").bitcast(F32)
+            nc.scalar.copy(
+                out=z_words.rearrange("p (v u) -> p v u", u=2),
+                in_=backs[c][:].rearrange("p (u v) -> p v u", u=2)[:, at : at + width, :],
+            )
 
         third = keep.tile([P, 2, V, 2], BF16, align_bytes=64)
         larger = keep.tile([P, 2, V, 2], BF16, align_bytes=64)
@@ -221,51 +226,52 @@ def tile_picked_pna_silu_p_kernel(
             nc.gpsimd.tensor_scalar(rounded[d][:], picked[0][d].rearrange("p e v -> p v e"), 1.0, 0.0, ALU.mult, ALU.add)
 
         def round_third(u, cols):
-            nc.vector.tensor_copy(out=third[:, u, cols], in_=last_list[:, u, :, cols].rearrange("p e v -> p v e"))
+            nc.vector.tensor_copy(
+                out=third[:, u, cols].rearrange("p (c i) e -> p c e i", i=LINE),
+                in_=last_list[:, u, :, cols].rearrange("p e (c i) -> p c e i", i=LINE),
+            )
 
         def first_pair_of_two(two, op):
             nc.vector.tensor_tensor(two[:, 0], rounded[0][:], rounded[1][:], op)
 
         def second_pair_of_two(two, op, cols):
-            first, second = (picked[1][d][:, :, cols].rearrange("p e v -> p v e") for d in range(2))
-            nc.vector.tensor_tensor(two[:, 1, cols], first, second, op)
+            first, second = (picked[1][d][:, :, cols].rearrange("p e (c i) -> p c e i", i=LINE) for d in range(2))
+            nc.vector.tensor_tensor(two[:, 1, cols].rearrange("p (c i) e -> p c e i", i=LINE), first, second, op)
 
         def with_third(a, two, op, c):
             nc.vector.tensor_tensor(
-                z_ends[c][:, a].rearrange("p v (u e) -> p v u e", u=2),
+                z[a][:, halves[c]].rearrange("p v (u e) -> p v u e", u=2),
                 two[:, :, halves[c]].rearrange("p u v e -> p v u e"),
                 third[:, :, halves[c]].rearrange("p u v e -> p v u e"),
                 op,
             )
 
-        accs = [bank() for b in range(3)]
-        groups = (((0, 0, HALF),), ((1, 0, P), (2, P, P)))
+        accs = [bank() for piece in pieces]
 
-        def second_product(values, matrices, c, start, stop):
-            width = len(matrices) * HALF
-            codes = keep.tile([P, width], U32, name="z_codes%d_%d" % (matrices[0], c), align_bytes=64)
-            scales = keep.tile([P, width], U8, name="z_scales%d_%d" % (matrices[0], c), align_bytes=64)
-            nc.vector.quantize_mx(out=codes[:].bitcast(FP8X4), scales=scales[:], in_=values)
-            for i, a in enumerate(matrices):
-                for g, at, cols in groups[c]:
-                    span = slice(i * HALF + at, i * HALF + at + cols)
-                    nc.tensor.matmul_mx(
-                        out=accs[g][:, 0:cols],
-                        lhsT=w_words[a][:].bitcast(FP4X4),
-                        lhsT_scale=w_scale_rows[:, a * N : (a + 1) * N],
-                        rhs=codes[:, span].bitcast(FP8X4),
-                        rhs_scale=scales[:, span],
-                        start=start and i == 0,
-                        stop=stop and i == len(matrices) - 1,
-                    )
+        def second_product(a, groups, start, stop):
+            first = pieces[groups[0]][0]
+            width = sum(pieces[g][1] for g in groups)
+            codes = keep.tile([P, width], U32, name="z_codes%d_%d" % (a, groups[0]), align_bytes=64)
+            scales = keep.tile([P, width], U8, name="z_scales%d_%d" % (a, groups[0]), align_bytes=64)
+            nc.vector.quantize_mx(
+                out=codes[:].bitcast(FP8X4),
+                scales=scales[:],
+                in_=z[a][:, first : first + width, :].rearrange("p v t -> p (v t)"),
+            )
+            for g in groups:
+                cols = slice(pieces[g][0] - first, pieces[g][0] - first + pieces[g][1])
+                nc.tensor.matmul_mx(
+                    out=accs[g][:, 0 : pieces[g][1]],
+                    lhsT=w_words[a][:].bitcast(FP4X4),
+                    lhsT_scale=w_scale_rows[:, a * N : (a + 1) * N],
+                    rhs=codes[:, cols].bitcast(FP8X4),
+                    rhs_scale=scales[:, cols],
+                    start=start,
+                    stop=stop,
+                )
 
-        def ends_product(c, start, stop):
-            second_product(z_ends[c][:].rearrange("p a v t -> p (a v t)"), (1, 2), c, start, stop)
-
-        def mean_product(c, start, stop):
-            second_product(z_mean[:, halves[c], :].rearrange("p v t -> p (v t)"), (0,), c, start, stop)
-
-        def store(g, first, width, copy):
+        def store(g, copy):
+            first, width = pieces[g]
             result = keep.tile([P, width], F32, name="result%d" % g, align_bytes=64)
             copy(out=result[:], in_=accs[g][:, 0:width])
             nc.sync.dma_start(out=out[:, first : first + width], in_=result[:])
@@ -277,15 +283,18 @@ def tile_picked_pna_silu_p_kernel(
         second_pair_of_two(smaller, ALU.min, halves[0])
         round_third(1, halves[0])
         second_pair_of_two(smaller, ALU.min, halves[1])
-        with_third(0, larger, ALU.max, 0)
-        with_third(1, smaller, ALU.min, 0)
+        with_third(1, larger, ALU.max, 0)
+        with_third(2, smaller, ALU.min, 0)
         round_third(1, halves[1])
-        ends_product(0, True, False)
-        with_third(0, larger, ALU.max, 1)
-        with_third(1, smaller, ALU.min, 1)
-        mean_product(0, False, True)
-        store(0, 0, HALF, nc.scalar.copy)
-        ends_product(1, True, False)
-        mean_product(1, False, True)
-        store(1, HALF, P, nc.scalar.copy)
-        store(2, HALF + P, P, nc.vector.tensor_copy)
+        second_product(1, (0,), True, False)
+        second_product(2, (0,), False, False)
+        with_third(1, larger, ALU.max, 1)
+        with_third(2, smaller, ALU.min, 1)
+        second_product(1, (1, 2), True, False)
+        second_product(0, (0,), False, True)
+        store(0, nc.scalar.copy)
+        second_product(2, (1, 2), False, False)
+        second_product(0, (1,), False, True)
+        store(1, nc.scalar.copy)
+        second_product(0, (2,), False, True)
+        store(2, nc.vector.tensor_copy)

@@ -49,6 +49,8 @@ def tile_picked_pna_silu_p_kernel(
         nc.vector.memset(x_scale_table[:].bitcast(I32), 0)
         identity = keep.tile([P, P], F32, align_bytes=64)
         nc.vector.memset(identity[:], 0.0)
+        warm = keep.tile([P, 1], F32, align_bytes=64)
+        nc.scalar.activation(out=warm[:], in_=identity[:, 0:1], func=ACT.Silu)
         make_identity(nc, identity[:], nomemset=True)
         x_scale_picked = keep.tile([P, S], U8, align_bytes=64)
         nc.vector.memset(x_scale_picked[:].bitcast(I32), 0)
@@ -68,13 +70,10 @@ def tile_picked_pna_silu_p_kernel(
             nc.sync.dma_start(out=rows[:], in_=w1.rearrange("(p j) c -> p j c", j=PACK)[:, 2 * i : 2 * i + 2, :])
             w1_raw.append(rows)
 
-        warm = keep.tile([P, 1], F32, align_bytes=64)
-        nc.scalar.activation(out=warm[:], in_=identity[:, 0:1], func=ACT.Silu)
-
         x_scale_gathered = keep.tile([P, S], U8, align_bytes=64)
         nc.vector.tensor_copy(x_scale_gathered[:], x_scale_table[:].indirect(offs_list[:]))
         for q in range(4):
-            nc.sync.dma_start(
+            nc.scalar.dma_start(
                 out=x_scale_picked[32 * q : 32 * q + 4, :].bitcast(I32),
                 in_=x_scale_gathered[32 + 16 * q : 48 + 16 * q : 4, :].bitcast(I32),
             )

from contextlib import ExitStack

import concourse.mybir as mybir
from concourse.masks import make_identity

K, T, S, V, H, N = 512, 4096, 1024, 512, 512, 128
FLOPS = 2 * K * H * S + 3 * 2 * H * N * V

F32 = mybir.dt.float32
BF16 = mybir.dt.bfloat16
I32 = mybir.dt.int32
U32 = mybir.dt.uint32
U16 = mybir.dt.uint16
U8 = mybir.dt.uint8
FP8X4 = mybir.dt.float8_e4m3fn_x4
FP4X4 = mybir.dt.float4_e2m1fn_x4
ACT = mybir.ActivationFunctionType
ALU = mybir.AluOpType

P = 128
PACK = 4
BANK = 512
HALF = V // 2
D = 3
LEAD = T // 4
LINE = 4


def load_scale_rows(queue, tile, rows):
    for r in range(4):
        queue.dma_start(out=tile[r:P:32, :].bitcast(I32), in_=rows[r:16:4, :].bitcast(I32))


def tile_picked_pna_silu_p_kernel(
    tc, x_words, x_scales, w1, w2_words, w2_scales, w3_words, w3_scales, w4_words, w4_scales, offs, pos1, pos2, pos3, out
):
    nc = tc.nc
    with ExitStack() as ctx:
        lists = ctx.enter_context(tc.tile_pool(name="lists", bufs=1))
        keep = ctx.enter_context(tc.tile_pool(name="keep", bufs=1))
        reuse = ctx.enter_context(tc.tile_pool(name="reuse", bufs=1))
        stage = ctx.enter_context(tc.tile_pool(name="stage", bufs=1))
        psum = ctx.enter_context(tc.psum_pool(name="psum", bufs=8))

        def bank():
            return psum.tile([P, BANK], F32, name="bank")

        x_scale_table = keep.tile([P, T], U8, align_bytes=64)
        nc.vector.memset(x_scale_table[:].bitcast(I32), 0)
        identity = keep.tile([P, P], F32, align_bytes=64)
        nc.vector.memset(identity[:], 0.0)
        warm = keep.tile([P, 1], F32, align_bytes=64)
        nc.scalar.activation(out=warm[:], in_=identity[:, 0:1], func=ACT.Silu)
        make_identity(nc, identity[:], nomemset=True)
        x_scale_picked = keep.tile([P, S], U8, align_bytes=64)
        nc.vector.memset(x_scale_picked[:].bitcast(I32), 0)
        w_scale_rows = keep.tile([P, D * N], U8, align_bytes=64)
        nc.vector.memset(w_scale_rows[:].bitcast(I32), 0)
        x_word_table = keep.tile([P, T], I32, align_bytes=64)
        x_word_rows = x_words[0].rearrange("p n t -> p (n t)").bitcast(I32)
        nc.sync.dma_start(out=x_word_table[:, 0:LEAD], in_=x_word_rows[:, 0:LEAD])
        offs_list = lists.tile([P, S // 16], U16, name="offs_list")
        nc.sync.dma_start(offs_list[:], offs)
        pos_lists = [lists.tile([P, V // 16], U16, name="pos_list%d" % d) for d in range(D)]
        nc.sync.dma_start(out=x_scale_table[32:96:4, :].bitcast(I32), in_=x_scales[0].bitcast(I32))
        nc.sync.dma_start(out=x_word_table[:, LEAD:T], in_=x_word_rows[:, LEAD:T])
        w1_raw = []
        for i in range(2):
            rows = reuse.tile([P, 2, H], F32, name="w1_raw%d" % i, align_bytes=64, offset=(1 - i) * 2 * H * 4)
            nc.sync.dma_start(out=rows[:], in_=w1.rearrange("(p j) c -> p j c", j=PACK)[:, 2 * i : 2 * i + 2, :])
            w1_raw.append(rows)

        x_scale_gathered = keep.tile([P, S], U8, align_bytes=64)
        nc.vector.tensor_copy(x_scale_gathered[:], x_scale_table[:].indirect(offs_list[:]))
        for q in range(4):
            nc.scalar.dma_start(
                out=x_scale_picked[32 * q : 32 * q + 4, :].bitcast(I32),
                in_=x_scale_gathered[32 + 16 * q : 48 + 16 * q : 4, :].bitcast(I32),
            )
        nc.sync.dma_start(pos_lists[0][:], pos1)
        nc.sync.dma_start(pos_lists[1][:], pos2)
        nc.sync.dma_start(pos_lists[2][:], pos3)
        x_picked = []
        for s in range(S // BANK):
            picked = keep.tile([P, BANK], U32, name="x_picked%d" % s, align_bytes=64)
            nc.vector.tensor_copy(
                picked[:], x_word_table[:].bitcast(U32).indirect(offs_list[:, s * BANK // 16 : (s + 1) * BANK // 16])
            )
            x_picked.append(picked)

        w1_bf = [
            stage.tile([P, n, P, PACK], BF16, name="w1_bf%d" % u, align_bytes=64, offset=at)
            for u, (n, at) in enumerate(((1, 0), (1, 4 * H), (2, 0)))
        ]
        w1_dealt = [rows[:].rearrange("p j (m t) -> p m t j", t=PACK) for rows in w1_raw]
        w1_codes = []
        w1_scales = []

        def round_w1(copy, u, i, ms):
            n = w1_bf[u].shape[1]
            copy(
                out=w1_bf[u][:].rearrange("p e m j -> p m e j")[:, ms, :, 2 * i : 2 * i + 2],
                in_=w1_dealt[i][:, ms, u : u + n, :],
            )

        def quantise_w1(u):
            n = w1_bf[u].shape[1]
            codes = keep.tile([P, n * P], U32, name="w1_codes%d" % u, align_bytes=64)
            scales = keep.tile([P, n * P], U8, name="w1_scales%d" % u, align_bytes=64)
            nc.vector.quantize_mx(
                out=codes[:].bitcast(FP8X4), scales=scales[:], in_=w1_bf[u][:].rearrange("p e m j -> p (e m j)")
            )
            for i in range(n):
                w1_codes.append(codes[:, i * P : (i + 1) * P])
                w1_scales.append(scales[:, i * P : (i + 1) * P])

        for u in range(2):
            round_w1(nc.scalar.copy, u, 0, slice(0, P))
        round_w1(nc.vector.tensor_copy, 0, 1, slice(0, P // 2))
        round_w1(nc.scalar.copy, 0, 1, slice(P // 2, P))
        round_w1(nc.scalar.copy, 1, 1, slice(0, P))
        quantise_w1(0)
        for i in range(2):
            round_w1(nc.vector.tensor_copy, 2, i, slice(0, P))
        quantise_w1(1)
        quantise_w1(2)

        w_words = []
        for a, (words, scales) in enumerate(((w2_words, w2_scales), (w3_words, w3_scales), (w4_words, w4_scales))):
            tile = keep.tile([P, 2 * N], U8, name="w_words%d" % a, align_bytes=64)
            nc.sync.dma_start(out=tile[:].bitcast(I32), in_=words[0].bitcast(I32))
            w_words.append(tile)
            load_scale_rows(nc.sync, w_scale_rows[:, a * N : (a + 1) * N], scales[0])

        h = []
        for t in range(PACK):
            h_t = keep.tile([P, S], F32, name="h%d" % t, align_bytes=64)
            pieces = ((0, 0, HALF), (0, HALF, HALF), (1, 0, HALF), (1, HALF, P), (1, HALF + P, P)) if t == 0 else ((0, 0, BANK), (1, 0, BANK))
            for s, first, width in pieces:
                acc = bank()
                cols = slice(s * BANK + first, s * BANK + first + width)
                nc.tensor.matmul_mx(
                    out=acc[:, 0:width],
                    lhsT=w1_codes[t].bitcast(FP8X4),
                    lhsT_scale=w1_scales[t],
                    rhs=x_picked[s][:, first : first + width].bitcast(FP8X4),
                    rhs_scale=x_scale_picked[:, cols],
                    start=True,
                    stop=True,
                )
                nc.scalar.activation(out=h_t[:, cols], in_=acc[:, 0:width], func=ACT.Silu)
            h.append(h_t)

        last_list = keep.tile([P, 2, 2, V], F32, align_bytes=64)
        picked = [
            [keep.tile([P, 2, V], F32, name="nbr%d_%d" % (u, d), align_bytes=64)[:] for d in range(2)] + [last_list[:, u]]
            for u in range(2)
        ]
        sums = [[bank(), bank()], [bank(), bank()]]
        added = {}

        def fetch(on_vector, t, d, first, width):
            u, e = divmod(t, 2)
            into = picked[u][d][:, e, first : first + width]
            found = h[t][:].indirect(pos_lists[d][:, first // 16 : (first + width) // 16])
            if on_vector:
                nc.vector.tensor_copy(into, found)
            else:
                nc.scalar.activation(out=into, in_=found, func=ACT.Copy)
            for b in range(first // P, (first + width) // P):
                count = added.get((u, b // 2), 0)
                added[(u, b // 2)] = count + 1
                place = (2 * (b % 2) + e) * P
                nc.tensor.matmul(
                    sums[u][b // 2][:, place : place + P],
                    picked[u][d][:, e, b * P : (b + 1) * P],
                    identity[:],
                    start=(count == 0),
                    stop=(count == 4 * D - 1),
                    is_transpose=True,
                )

        for t, d in ((0, 0), (0, 1), (1, 0), (1, 1), (2, 0)):
            fetch(True, t, d, 0, V)
        fetch(True, 3, 0, 0, V - P)
        fetch(False, 3, 0, V - P, P)
        for t, d in ((2, 1), (3, 1), (0, 2), (1, 2)):
            fetch(False, t, d, 0, V)
        for first in (0, HALF):
            for t in (2, 3):
                fetch(False, t, 2, first, HALF)

        z = [keep.tile([P, V, PACK], BF16, name="z%d" % a, align_bytes=64) for a in range(D)]
        backs = []
        for c in range(2):
            back = bank()
            for u in range(2):
                turned = keep.tile([P, 2, P, 2], BF16, name="mean_turned%d_%d" % (u, c), align_bytes=64)
                nc.scalar.activation(
                    out=turned[:],
                    in_=sums[u][c][:].rearrange("v (b e p) -> v b p e", b=2, e=2),
                    func=ACT.Copy,
                    scale=1.0 / D,
                )
                words = turned[:].rearrange("v b p e -> v (b p e)").bitcast(F32)
                for b in range(2):
                    place = (2 * u + b) * P
                    nc.tensor.transpose(back[:, place : place + P], words[:, b * P : (b + 1) * P], identity[:])
            backs.append(back)
        halves = (slice(0, HALF), slice(HALF, V))
        pieces = ((0, HALF), (HALF, P), (HALF + P, P))
        for first, width in pieces:
            c, at = divmod(first, HALF)
            z_words = z[0][:, first : first + width, :].rearrange("p v t -> p (v t)").bitcast(F32)
            nc.scalar.copy(
                out=z_words.rearrange("p (v u) -> p v u", u=2),
                in_=backs[c][:].rearrange("p (u v) -> p v u", u=2)[:, at : at + width, :],
            )

        third = keep.tile([P, 2, V, 2], BF16, align_bytes=64)
        larger = keep.tile([P, 2, V, 2], BF16, align_bytes=64)
        smaller = keep.tile([P, 2, V, 2], BF16, align_bytes=64)
        rounded = [keep.tile([P, V, 2], BF16, name="rounded%d" % d, align_bytes=64) for d in range(2)]
        for d in range(2):
            nc.gpsimd.tensor_scalar(rounded[d][:], picked[0][d].rearrange("p e v -> p v e"), 1.0, 0.0, ALU.mult, ALU.add)

        def round_third(u, cols):
            nc.vector.tensor_copy(
                out=third[:, u, cols].rearrange("p (c i) e -> p c e i", i=LINE),
                in_=last_list[:, u, :, cols].rearrange("p e (c i) -> p c e i", i=LINE),
            )

        def first_pair_of_two(two, op):
            nc.vector.tensor_tensor(two[:, 0], rounded[0][:], rounded[1][:], op)

        def second_pair_of_two(two, op, cols):
            first, second = (picked[1][d][:, :, cols].rearrange("p e (c i) -> p c e i", i=LINE) for d in range(2))
            nc.vector.tensor_tensor(two[:, 1, cols].rearrange("p (c i) e -> p c e i", i=LINE), first, second, op)

        def with_third(a, two, op, c):
            nc.vector.tensor_tensor(
                z[a][:, halves[c]].rearrange("p v (u e) -> p v u e", u=2),
                two[:, :, halves[c]].rearrange("p u v e -> p v u e"),
                third[:, :, halves[c]].rearrange("p u v e -> p v u e"),
                op,
            )

        accs = [bank() for piece in pieces]

        def second_product(a, groups, start, stop):
            first = pieces[groups[0]][0]
            width = sum(pieces[g][1] for g in groups)
            codes = keep.tile([P, width], U32, name="z_codes%d_%d" % (a, groups[0]), align_bytes=64)
            scales = keep.tile([P, width], U8, name="z_scales%d_%d" % (a, groups[0]), align_bytes=64)
            nc.vector.quantize_mx(
                out=codes[:].bitcast(FP8X4),
                scales=scales[:],
                in_=z[a][:, first : first + width, :].rearrange("p v t -> p (v t)"),
            )
            for g in groups:
                cols = slice(pieces[g][0] - first, pieces[g][0] - first + pieces[g][1])
                nc.tensor.matmul_mx(
                    out=accs[g][:, 0 : pieces[g][1]],
                    lhsT=w_words[a][:].bitcast(FP4X4),
                    lhsT_scale=w_scale_rows[:, a * N : (a + 1) * N],
                    rhs=codes[:, cols].bitcast(FP8X4),
                    rhs_scale=scales[:, cols],
                    start=start,
                    stop=stop,
                )

        def store(g, copy):
            first, width = pieces[g]
            result = keep.tile([P, width], F32, name="result%d" % g, align_bytes=64)
            copy(out=result[:], in_=accs[g][:, 0:width])
            nc.sync.dma_start(out=out[:, first : first + width], in_=result[:])

        first_pair_of_two(larger, ALU.max)
        first_pair_of_two(smaller, ALU.min)
        second_pair_of_two(larger, ALU.max, slice(0, V))
        round_third(0, slice(0, V))
        second_pair_of_two(smaller, ALU.min, halves[0])
        round_third(1, halves[0])
        second_pair_of_two(smaller, ALU.min, halves[1])
        with_third(1, larger, ALU.max, 0)
        with_third(2, smaller, ALU.min, 0)
        round_third(1, halves[1])
        second_product(1, (0,), True, False)
        second_product(2, (0,), False, False)
        with_third(1, larger, ALU.max, 1)
        with_third(2, smaller, ALU.min, 1)
        second_product(1, (1, 2), True, False)
        second_product(0, (0,), False, True)
        store(0, nc.scalar.copy)
        second_product(2, (1, 2), False, False)
        second_product(0, (1,), False, True)
        store(1, nc.scalar.copy)
        second_product(0, (2,), False, True)
        store(2, nc.vector.tensor_copy)
